import numpy as np
import ml_dtypes


def mxq(x, axis, fmt="e4m3"):
    dtype, down = {"e4m3": (ml_dtypes.float8_e4m3fn, 7), "e5m2": (ml_dtypes.float8_e5m2, 14)}[fmt]
    v = np.moveaxis(np.asarray(x, np.float32).astype(ml_dtypes.bfloat16).astype(np.float64), axis, -1)
    blocks = v.reshape(v.shape[:-1] + (-1, 32))
    amax = np.abs(blocks).max(-1, keepdims=True)
    byte = np.maximum(np.where(amax > 0, np.frexp(amax)[1] - 1 + 127, 0) - down, 1)
    scale = np.exp2(byte - 127.0)
    codes = (blocks / scale).astype(np.float32).astype(dtype).astype(np.float64)
    return np.moveaxis((codes * scale).reshape(v.shape), -1, axis)


WIDE = False


def mx_kscale(k):
    if not WIDE:
        return np.ones(k)
    levels = np.array([10, -10, 5, -5, 0])
    if k % 512:
        return np.exp2(np.random.permutation(np.resize(levels, k // 32))).repeat(32)
    a = np.empty((k // 512, 16))
    for p in range(k // 512):
        a[p, :8] = np.random.permutation(np.resize(levels, 8))
        for g in range(8):
            far = levels[np.abs(levels - a[p, g]) >= 10]
            a[p, g + 8] = far[np.random.randint(len(far))]
    return np.exp2(a.ravel()).repeat(32)


def f64(x):
    return np.asarray(x).astype(np.float64)


def striped(idx):
    return np.tile(np.asarray(idx).reshape(-1, 16).T, (8, 1)).astype(np.uint16)


def unstriped(offs):
    return offs[:16].T.reshape(-1).astype(np.int64)


E2M1 = np.array([0.0, 0.5, 1.0, 1.5, 2.0, 3.0, 4.0, 6.0, -0.0, -0.5, -1.0, -1.5, -2.0, -3.0, -4.0, -6.0])


def pack_weight(w, fmt):
    k, n = w.shape
    w = f64(np.asarray(w, np.float32).astype(ml_dtypes.bfloat16)).reshape(k // 32, 32, n)
    amax = np.abs(w).max(1)
    if fmt == "e4m3":
        byte = np.frexp(amax)[1] - 1 + 127 - 7
    else:
        mant, ex = np.frexp(amax / 6.0)
        byte = np.where(mant > 0.5, ex, ex - 1) + 127
    byte = np.clip(np.where(amax > 0, byte, 1), 1, 254)
    scaled = (w * np.exp2(127.0 - byte)[:, None, :]).reshape(k, n).astype(np.float32)
    by_word = np.ascontiguousarray(scaled.reshape(k // 512, 128, 4, n).transpose(0, 1, 3, 2))
    if fmt == "e4m3":
        words = by_word.astype(ml_dtypes.float8_e4m3fn).view(np.uint8)
    else:
        c = by_word.astype(ml_dtypes.float4_e2m1fn).view(np.uint8) & 0xF
        words = (c[..., 0::2] | (c[..., 1::2] << 4)).reshape(k // 512, 128, 2 * n)
    return np.ascontiguousarray(words), np.ascontiguousarray(byte.astype(np.uint8).reshape(k // 512, 16, n))


def unpack_weight(words, scales, fmt):
    g, _, n = scales.shape
    words = np.ascontiguousarray(words).reshape(g, 128, n, -1)
    if fmt == "e4m3":
        vals = words.view(ml_dtypes.float8_e4m3fn).astype(np.float64)
    else:
        nib = np.empty((g, 128, n, 4), np.uint8)
        nib[..., 0::2] = words & 0xF
        nib[..., 1::2] = words >> 4
        vals = E2M1[nib]
    vals = vals * np.repeat(np.exp2(scales.astype(np.float64) - 127.0), 8, axis=1)[..., None]
    return vals.transpose(0, 1, 3, 2).reshape(g * 512, n)


D, T, I, M, E = 512, 2048, 512, 512, 512


def setup_inputs():
    n = np.random.standard_normal
    idx = np.random.permutation(T)[:I]
    fd = mx_kscale(D)
    fm = mx_kscale(M)
    tokp = pack_weight(n((D, T)) / fd[:, None], "e2m1")
    return {
        "tok_words": tokp[0],
        "tok_scales": tokp[1],
        "mk": (n((D, M)) * 0.5 / np.sqrt(D) * fd[:, None]).astype(np.float32),
        "msc": (np.random.uniform(8.0, 24.0, (M, 1)) * fm[:, None]).astype(np.float32),
        "mv": (n((M, E)) / fm[:, None]).astype(np.float32),
        "offs": striped(idx),
    }


def reference(tok_words, tok_scales, mk, msc, mv, offs):
    idx = unstriped(offs)
    toku = unpack_weight(tok_words, tok_scales, "e2m1")
    mkq = mxq(f64(mk), 0, "e4m3")
    tokidxg = toku[:, idx]
    a = mkq.T @ tokidxg
    p = np.exp(a - np.max(a, axis=1, keepdims=True))
    s = p / np.sum(p, axis=1, keepdims=True)
    st = s.T
    x = st / np.sum(st, axis=1, keepdims=True)
    xt = x.T
    w = xt * f64(msc)
    mvq = mxq(f64(mv), 0, "e4m3")
    wq = mxq(w, 0, "e4m3")
    y = mvq.T @ wq
    return y

@@ -1,0 +1,201 @@
+from contextlib import ExitStack
+
+import concourse.mybir as mybir
+from concourse.masks import make_identity
+
+D, T, I, M, E = 512, 2048, 512, 512, 512
+FLOPS = 2 * D * M * I + 2 * M * E * I
+
+F32 = mybir.dt.float32
+BF16 = mybir.dt.bfloat16
+I32 = mybir.dt.int32
+U32 = mybir.dt.uint32
+U16 = mybir.dt.uint16
+U8 = mybir.dt.uint8
+FP8X4 = mybir.dt.float8_e4m3fn_x4
+FP4X4 = mybir.dt.float4_e2m1fn_x4
+ALU = mybir.AluOpType
+ACT = mybir.ActivationFunctionType
+AX = mybir.AxisListType
+
+P = 128
+PACK = 4
+CHUNK = 128
+CHUNKS = I // CHUNK
+
+
+def tile_attend_externalattn_kernel(tc, tok_words, tok_scales, mk, msc, mv, offs, out):
+    nc = tc.nc
+    with ExitStack() as ctx:
+        keep = ctx.enter_context(tc.tile_pool(name="keep", bufs=1))
+        psum = ctx.enter_context(tc.psum_pool(name="psum", bufs=1))
+
+        def sb(name, shape, dtype, tag=None):
+            return keep.tile(shape, dtype, name=name, tag=tag or name, align_bytes=64)
+
+        def bank(name, shape, k):
+            return psum.tile(shape, F32, name=name, tag="bank%d" % k)
+
+        offsets = keep.tile([P, I // 16], U16, name="offsets")
+        nc.sync.dma_start(offsets[:], offs)
+        msc_sb = sb("msc_sb", [P, PACK], F32)
+        nc.sync.dma_start(msc_sb[:], msc.rearrange("(p r) o -> p (r o)", r=PACK))
+        pool_scales = sb("pool_scales", [P, T], U8)
+        nc.gpsimd.memset(pool_scales[:].bitcast(I32), 0)
+        for q in range(4):
+            nc.sync.dma_start(
+                pool_scales[32 * q : 32 * q + 4, :].bitcast(I32),
+                tok_scales[0, 4 * q : 4 * q + 4, :].bitcast(I32),
+            )
+        pool_words = sb("pool_words", [P, T], U16)
+        nc.sync.dma_start(pool_words[:].bitcast(I32), tok_words[0].bitcast(I32))
+        mk_rows = mk.rearrange("(p j) m -> p j m", j=PACK)
+        mk_raw = []
+        for h in range(2):
+            raw = sb("mk_raw%d" % h, [P, PACK, M // 2], F32)
+            nc.sync.dma_start(raw[:], mk_rows[:, :, h * 256 : (h + 1) * 256])
+            mk_raw.append(raw)
+        mv_raw = sb("mv_raw", [P, PACK, E], F32)
+        nc.sync.dma_start(mv_raw[:], mv.rearrange("(p j) e -> p j e", j=PACK))
+
+        ident = sb("ident", [P, P], F32)
+        make_identity(nc, ident[:])
+        warm = sb("warm", [P, 1], F32)
+        nc.scalar.activation(warm[:], ident[:, 0:1], ACT.Exp)
+
+        tok_s = sb("tok_s", [P, I], U8)
+        nc.vector.tensor_copy(tok_s[:], pool_scales[:].indirect(offsets[:]))
+        tok_w = sb("tok_w", [P, I], U16)
+        nc.vector.tensor_copy(tok_w[:], pool_words[:].indirect(offsets[:]))
+
+        mk_codes = [sb("mk_codes%d" % r, [P, P], U32) for r in range(PACK)]
+        mk_scales = [sb("mk_scales%d" % r, [P, P], U8) for r in range(PACK)]
+        for h in range(2):
+            by_place = mk_raw[h][:].rearrange("p j (s r) -> p s j r", r=PACK)
+            for pair in range(2):
+                grouped = sb("mk_grouped%d%d" % (h, pair), [P, 2, 64, PACK], BF16)
+                dst = grouped[:].rearrange("p r s j -> p s j r")
+                src = by_place[:, :, :, 2 * pair : 2 * pair + 2]
+                if pair == 0:
+                    nc.vector.tensor_copy(dst, src)
+                else:
+                    nc.scalar.copy(dst, src)
+                for rr in range(2):
+                    r = 2 * pair + rr
+                    nc.vector.quantize_mx(
+                        out=mk_codes[r][:, 64 * h : 64 * h + 64].bitcast(FP8X4),
+                        scales=mk_scales[r][:, 64 * h : 64 * h + 64],
+                        in_=grouped[:, rr].rearrange("p s j -> p (s j)"),
+                    )
+
+        p_sb = [sb("p%d" % r, [P, I], F32) for r in range(PACK)]
+        row_sum = sb("row_sum", [P, PACK - 1], F32)
+        row_sum_last = sb("row_sum_last", [P, 1], F32, tag="late_b")
+        for r in range(PACK):
+            scores = bank("scores%d" % r, [P, I], r)
+            nc.tensor.matmul_mx(
+                out=scores[:],
+                lhsT=mk_codes[r][:].bitcast(FP8X4),
+                lhsT_scale=mk_scales[r][:],
+                rhs=tok_w[:].bitcast(FP4X4),
+                rhs_scale=tok_s[:],
+                start=True,
+                stop=True,
+            )
+            last = r == PACK - 1
+            neg_max = sb("neg_max%d" % r, [P, 1], F32, tag="late_a" if last else None)
+            nc.vector.tensor_reduce(neg_max[:], scores[:], AX.X, ALU.max, negate=True)
+            nc.scalar.activation(
+                p_sb[r][:], scores[:], ACT.Exp, bias=neg_max[:], scale=1.0,
+                accum_out=row_sum_last[:] if last else row_sum[:, r : r + 1],
+            )
+
+        row_inv = sb("row_inv", [P, PACK - 1], F32)
+        nc.vector.reciprocal(row_inv[:], row_sum[:])
+        factor = sb("factor", [P, 2], F32)
+        nc.vector.tensor_tensor(factor[:], row_inv[:, 0:2], msc_sb[:, 0:2], ALU.mult)
+        row_inv_last = sb("row_inv_last", [P, 1], F32)
+        nc.vector.reciprocal(row_inv_last[:], row_sum_last[:])
+        inv = [row_inv[:, 0:1], row_inv[:, 1:2], row_inv[:, 2:3], row_inv_last[:]]
+        s_sb = [sb("s%d" % r, [P, I], F32) for r in range(PACK)]
+        for r in range(PACK):
+            nc.vector.tensor_scalar(s_sb[r][:], p_sb[r][:], inv[r], None, ALU.mult)
+
+        spread = []
+        for c in range(CHUNKS):
+            cols = slice(c * CHUNK, (c + 1) * CHUNK)
+            turned = bank("turned%d" % c, [P, P], 4 + c)
+            for r in range(PACK):
+                nc.tensor.matmul(turned[:], s_sb[r][:, cols], ident[:], start=(r == 0), stop=(r == PACK - 1), is_transpose=True)
+            col_sum = sb("col_sum%d" % c, [P, 1], F32)
+            nc.vector.tensor_reduce(col_sum[:], turned[:], AX.X, ALU.add)
+            col_inv = sb("col_inv%d" % c, [P, 1], F32)
+            nc.vector.reciprocal(col_inv[:], col_sum[:])
+            wide = bank("spread%d" % c, [P, CHUNK], c)
+            nc.tensor.transpose(wide[:], col_inv[:].to_broadcast([P, P]), ident[:])
+            spread.append(wide)
+
+        scaled = sb("scaled", [P, PACK, I], F32)
+        for r in range(2):
+            nc.scalar.activation(scaled[:, r, :], p_sb[r][:], ACT.Copy, scale=factor[:, r : r + 1])
+        for r in range(2, PACK):
+            nc.vector.tensor_scalar(scaled[:, r, :], p_sb[r][:], inv[r], msc_sb[:, r : r + 1], ALU.mult, ALU.mult)
+
+        mv_codes = [None] * PACK
+        mv_scales = [None] * PACK
+        mv_grouped = sb("mv_grouped01", [P, 256, PACK], BF16)
+        nc.gpsimd.tensor_scalar(
+            mv_grouped[:],
+            mv_raw[:, :, 0:256].rearrange("p j e -> p e j"),
+            1.0, 0.0, ALU.mult, ALU.add,
+        )
+        codes01 = sb("mv_codes01", [P, 256], U32)
+        scales01 = sb("mv_scales01", [P, 256], U8)
+        nc.vector.quantize_mx(out=codes01[:].bitcast(FP8X4), scales=scales01[:], in_=mv_grouped[:].rearrange("p e j -> p (e j)"))
+        for b in range(2):
+            mv_codes[b] = codes01[:, b * P : (b + 1) * P]
+            mv_scales[b] = scales01[:, b * P : (b + 1) * P]
+        for b in range(2, 4):
+            grouped = sb("mv_grouped%d" % b, [P, P, PACK], BF16, tag="late_a" if b == 2 else "late_b")
+            nc.scalar.copy(
+                grouped[:].rearrange("p (c i) j -> p c j i", i=4),
+                mv_raw[:, :, b * P : (b + 1) * P].rearrange("p j (c i) -> p c j i", i=4),
+            )
+            codes = sb("mv_codes%d" % b, [P, P], U32)
+            scales = sb("mv_scales%d" % b, [P, P], U8)
+            nc.vector.quantize_mx(out=codes[:].bitcast(FP8X4), scales=scales[:], in_=grouped[:].rearrange("p e j -> p (e j)"))
+            mv_codes[b] = codes[:]
+            mv_scales[b] = scales[:]
+
+        out_rows = out.rearrange("(b p) i -> p b i", p=P)
+        for c in range(CHUNKS):
+            cols = slice(c * CHUNK, (c + 1) * CHUNK)
+            w = sb("w%d" % c, [P, CHUNK, PACK], BF16)
+            nc.vector.tensor_tensor(
+                w[:].rearrange("p (g i) r -> p g r i", i=4),
+                scaled[:, :, cols].rearrange("p r (g i) -> p g r i", i=4),
+                spread[c][:].rearrange("p (g i) -> p g i", i=4).unsqueeze(2).to_broadcast([P, CHUNK // 4, PACK, 4]),
+                ALU.mult,
+            )
+            w_codes = sb("w_codes%d" % c, [P, CHUNK], U32)
+            w_scales = sb("w_scales%d" % c, [P, CHUNK], U8)
+            nc.vector.quantize_mx(out=w_codes[:].bitcast(FP8X4), scales=w_scales[:], in_=w[:].rearrange("p i r -> p (i r)"))
+            parts = [(0, 4, 4 + c)] if c < CHUNKS - 1 else [(0, 2, 4 + c), (2, 4, 0)]
+            for k, (b0, b1, bk) in enumerate(parts):
+                acc = bank("acc%d_%d" % (c, k), [P, b1 - b0, CHUNK], bk)
+                for b in range(b0, b1):
+                    nc.tensor.matmul_mx(
+                        out=acc[:, b - b0, :],
+                        lhsT=mv_codes[b].bitcast(FP8X4),
+                        lhsT_scale=mv_scales[b],
+                        rhs=w_codes[:].bitcast(FP8X4),
+                        rhs_scale=w_scales[:],
+                        start=True,
+                        stop=True,
+                    )
+                result = sb("result%d_%d" % (c, k), [P, b1 - b0, CHUNK], F32)
+                if k == 0:
+                    nc.scalar.copy(result[:], acc[:])
+                else:
+                    nc.vector.tensor_copy(result[:], acc[:])
+                nc.sync.dma_start(out_rows[:, b0:b1, cols], result[:])

@@ -38,8 +38,8 @@ def tile_attend_externalattn_kernel(tc, tok_words, tok_scales, mk, msc, mv, offs
 
         offsets = keep.tile([P, I // 16], U16, name="offsets")
         nc.sync.dma_start(offsets[:], offs)
-        msc_sb = sb("msc_sb", [P, PACK], F32)
-        nc.sync.dma_start(msc_sb[:], msc.rearrange("(p r) o -> p (r o)", r=PACK))
+        pool_words = sb("pool_words", [P, T], U16)
+        nc.sync.dma_start(pool_words[:].bitcast(I32), tok_words[0].bitcast(I32))
         pool_scales = sb("pool_scales", [P, T], U8)
         nc.gpsimd.memset(pool_scales[:].bitcast(I32), 0)
         for q in range(4):
@@ -47,50 +47,56 @@ def tile_attend_externalattn_kernel(tc, tok_words, tok_scales, mk, msc, mv, offs
                 pool_scales[32 * q : 32 * q + 4, :].bitcast(I32),
                 tok_scales[0, 4 * q : 4 * q + 4, :].bitcast(I32),
             )
-        pool_words = sb("pool_words", [P, T], U16)
-        nc.sync.dma_start(pool_words[:].bitcast(I32), tok_words[0].bitcast(I32))
         mk_rows = mk.rearrange("(p j) m -> p j m", j=PACK)
         mk_raw = []
         for h in range(2):
             raw = sb("mk_raw%d" % h, [P, PACK, M // 2], F32)
             nc.sync.dma_start(raw[:], mk_rows[:, :, h * 256 : (h + 1) * 256])
             mk_raw.append(raw)
-        mv_raw = sb("mv_raw", [P, PACK, E], F32)
-        nc.sync.dma_start(mv_raw[:], mv.rearrange("(p j) e -> p j e", j=PACK))
+        mv_rows = mv.rearrange("(p j) e -> p j e", j=PACK)
+        mv_raw = []
+        for h in range(2):
+            raw = sb("mv_raw%d" % h, [P, PACK, E // 2], F32)
+            nc.sync.dma_start(raw[:], mv_rows[:, :, h * 256 : (h + 1) * 256])
+            mv_raw.append(raw)
+        msc_sb = sb("msc_sb", [P, PACK], F32)
+        nc.sync.dma_start(msc_sb[:], msc.rearrange("(p r) o -> p (r o)", r=PACK))
 
         ident = sb("ident", [P, P], F32)
         make_identity(nc, ident[:])
         warm = sb("warm", [P, 1], F32)
         nc.scalar.activation(warm[:], ident[:, 0:1], ACT.Exp)
 
-        tok_s = sb("tok_s", [P, I], U8)
-        nc.vector.tensor_copy(tok_s[:], pool_scales[:].indirect(offsets[:]))
         tok_w = sb("tok_w", [P, I], U16)
         nc.vector.tensor_copy(tok_w[:], pool_words[:].indirect(offsets[:]))
+        tok_s = sb("tok_s", [P, I], U8)
+        nc.vector.tensor_copy(tok_s[:], pool_scales[:].indirect(offsets[:]))
 
         mk_codes = [sb("mk_codes%d" % r, [P, P], U32) for r in range(PACK)]
         mk_scales = [sb("mk_scales%d" % r, [P, P], U8) for r in range(PACK)]
-        for h in range(2):
-            by_place = mk_raw[h][:].rearrange("p j (s r) -> p s j r", r=PACK)
-            for pair in range(2):
-                grouped = sb("mk_grouped%d%d" % (h, pair), [P, 2, 64, PACK], BF16)
-                dst = grouped[:].rearrange("p r s j -> p s j r")
+        for pair in range(2):
+            grouped = sb("mk_grouped%d" % pair, [P, 2, P, PACK], BF16)
+            for h in range(2):
+                by_place = mk_raw[h][:].rearrange("p j (s r) -> p s j r", r=PACK)
+                dst = grouped[:, :, 64 * h : 64 * h + 64, :].rearrange("p r s j -> p s j r")
                 src = by_place[:, :, :, 2 * pair : 2 * pair + 2]
-                if pair == 0:
+                if (pair, h) == (0, 1):
                     nc.vector.tensor_copy(dst, src)
                 else:
                     nc.scalar.copy(dst, src)
-                for rr in range(2):
-                    r = 2 * pair + rr
-                    nc.vector.quantize_mx(
-                        out=mk_codes[r][:, 64 * h : 64 * h + 64].bitcast(FP8X4),
-                        scales=mk_scales[r][:, 64 * h : 64 * h + 64],
-                        in_=grouped[:, rr].rearrange("p s j -> p (s j)"),
-                    )
+            for rr in range(2):
+                r = 2 * pair + rr
+                nc.vector.quantize_mx(
+                    out=mk_codes[r][:].bitcast(FP8X4),
+                    scales=mk_scales[r][:],
+                    in_=grouped[:, rr].rearrange("p s j -> p (s j)"),
+                )
 
         p_sb = [sb("p%d" % r, [P, I], F32) for r in range(PACK)]
-        row_sum = sb("row_sum", [P, PACK - 1], F32)
-        row_sum_last = sb("row_sum_last", [P, 1], F32, tag="late_b")
+        row_sum01 = sb("row_sum01", [P, 2], F32)
+        row_sum2 = sb("row_sum2", [P, 1], F32)
+        row_sum3 = sb("row_sum3", [P, 1], F32, tag="late_b")
+        row_sum = [row_sum01[:, 0:1], row_sum01[:, 1:2], row_sum2[:], row_sum3[:]]
         for r in range(PACK):
             scores = bank("scores%d" % r, [P, I], r)
             nc.tensor.matmul_mx(
@@ -107,82 +113,104 @@ def tile_attend_externalattn_kernel(tc, tok_words, tok_scales, mk, msc, mv, offs
             nc.vector.tensor_reduce(neg_max[:], scores[:], AX.X, ALU.max, negate=True)
             nc.scalar.activation(
                 p_sb[r][:], scores[:], ACT.Exp, bias=neg_max[:], scale=1.0,
-                accum_out=row_sum_last[:] if last else row_sum[:, r : r + 1],
+                accum_out=row_sum[r],
             )
 
-        row_inv = sb("row_inv", [P, PACK - 1], F32)
-        nc.vector.reciprocal(row_inv[:], row_sum[:])
-        factor = sb("factor", [P, 2], F32)
-        nc.vector.tensor_tensor(factor[:], row_inv[:, 0:2], msc_sb[:, 0:2], ALU.mult)
-        row_inv_last = sb("row_inv_last", [P, 1], F32)
-        nc.vector.reciprocal(row_inv_last[:], row_sum_last[:])
-        inv = [row_inv[:, 0:1], row_inv[:, 1:2], row_inv[:, 2:3], row_inv_last[:]]
-        s_sb = [sb("s%d" % r, [P, I], F32) for r in range(PACK)]
-        for r in range(PACK):
-            nc.vector.tensor_scalar(s_sb[r][:], p_sb[r][:], inv[r], None, ALU.mult)
+        row_inv = sb("row_inv", [P, PACK], F32)
+        factor = sb("factor", [P, PACK], F32)
+        inv = [row_inv[:, r : r + 1] for r in range(PACK)]
+        fac = [factor[:, r : r + 1] for r in range(PACK)]
+        shares = {}
 
+        def share(r, c0, c1):
+            t = sb("share%d_%d" % (r, c0), [P, (c1 - c0) * CHUNK], F32)
+            nc.vector.tensor_scalar(t[:], p_sb[r][:, c0 * CHUNK : c1 * CHUNK], inv[r], None, ALU.mult)
+            for c in range(c0, c1):
+                shares[(r, c)] = t[:, (c - c0) * CHUNK : (c - c0 + 1) * CHUNK]
+
+        nc.vector.reciprocal(row_inv[:, 0:2], row_sum01[:])
+        nc.vector.tensor_tensor(factor[:, 0:2], row_inv[:, 0:2], msc_sb[:, 0:2], ALU.mult)
+        nc.vector.reciprocal(inv[2], row_sum[2])
+        nc.vector.reciprocal(inv[3], row_sum[3])
+        share(3, 0, 1)
+        share(2, 0, 1)
+        share(0, 0, 4)
+        share(1, 0, 4)
+        nc.vector.tensor_tensor(factor[:, 2:4], row_inv[:, 2:4], msc_sb[:, 2:4], ALU.mult)
+        share(2, 1, 4)
+        share(3, 1, 4)
+
+        scaled = [sb("scaled%d" % h, [P, PACK, I // 2], F32) for h in range(2)]
+
+        def scale_half(h):
+            for r in range(PACK):
+                nc.scalar.activation(scaled[h][:, r, :], p_sb[r][:, h * 256 : (h + 1) * 256], ACT.Copy, scale=fac[r])
+
+        scale_half(0)
+
+        turned = []
+        for c in range(CHUNKS):
+            t = bank("turned%d" % c, [P, P], 4 + c)
+            for r in range(PACK):
+                nc.tensor.matmul(t[:], shares[(r, c)], ident[:], start=(r == 0), stop=(r == PACK - 1), is_transpose=True)
+            turned.append(t)
+        col_inv = []
+        for c in range(2):
+            col_sum = sb("col_sum%d" % c, [P, 1], F32)
+            nc.vector.tensor_reduce(col_sum[:], turned[c][:], AX.X, ALU.add)
+            one = sb("col_inv%d" % c, [P, 1], F32)
+            nc.vector.reciprocal(one[:], col_sum[:])
+            col_inv.append(one[:])
+        col_sum23 = sb("col_sum23", [P, 2], F32)
+        for c in range(2, 4):
+            spent = sb("spent%d" % c, [P, P], F32)
+            nc.scalar.activation(spent[:], turned[c][:], ACT.Copy, accum_out=col_sum23[:, c - 2 : c - 1])
+        col_inv23 = sb("col_inv23", [P, 2], F32)
+        nc.vector.reciprocal(col_inv23[:], col_sum23[:])
+        col_inv.extend([col_inv23[:, 0:1], col_inv23[:, 1:2]])
         spread = []
         for c in range(CHUNKS):
-            cols = slice(c * CHUNK, (c + 1) * CHUNK)
-            turned = bank("turned%d" % c, [P, P], 4 + c)
-            for r in range(PACK):
-                nc.tensor.matmul(turned[:], s_sb[r][:, cols], ident[:], start=(r == 0), stop=(r == PACK - 1), is_transpose=True)
-            col_sum = sb("col_sum%d" % c, [P, 1], F32)
-            nc.vector.tensor_reduce(col_sum[:], turned[:], AX.X, ALU.add)
-            col_inv = sb("col_inv%d" % c, [P, 1], F32)
-            nc.vector.reciprocal(col_inv[:], col_sum[:])
             wide = bank("spread%d" % c, [P, CHUNK], c)
-            nc.tensor.transpose(wide[:], col_inv[:].to_broadcast([P, P]), ident[:])
+            nc.tensor.transpose(wide[:], col_inv[c].to_broadcast([P, P]), ident[:])
             spread.append(wide)
+        scale_half(1)
 
-        scaled = sb("scaled", [P, PACK, I], F32)
-        for r in range(2):
-            nc.scalar.activation(scaled[:, r, :], p_sb[r][:], ACT.Copy, scale=factor[:, r : r + 1])
-        for r in range(2, PACK):
-            nc.vector.tensor_scalar(scaled[:, r, :], p_sb[r][:], inv[r], msc_sb[:, r : r + 1], ALU.mult, ALU.mult)
-
-        mv_codes = [None] * PACK
-        mv_scales = [None] * PACK
-        mv_grouped = sb("mv_grouped01", [P, 256, PACK], BF16)
-        nc.gpsimd.tensor_scalar(
-            mv_grouped[:],
-            mv_raw[:, :, 0:256].rearrange("p j e -> p e j"),
-            1.0, 0.0, ALU.mult, ALU.add,
-        )
-        codes01 = sb("mv_codes01", [P, 256], U32)
-        scales01 = sb("mv_scales01", [P, 256], U8)
-        nc.vector.quantize_mx(out=codes01[:].bitcast(FP8X4), scales=scales01[:], in_=mv_grouped[:].rearrange("p e j -> p (e j)"))
-        for b in range(2):
-            mv_codes[b] = codes01[:, b * P : (b + 1) * P]
-            mv_scales[b] = scales01[:, b * P : (b + 1) * P]
-        for b in range(2, 4):
-            grouped = sb("mv_grouped%d" % b, [P, P, PACK], BF16, tag="late_a" if b == 2 else "late_b")
-            nc.scalar.copy(
-                grouped[:].rearrange("p (c i) j -> p c j i", i=4),
-                mv_raw[:, :, b * P : (b + 1) * P].rearrange("p j (c i) -> p c j i", i=4),
-            )
-            codes = sb("mv_codes%d" % b, [P, P], U32)
-            scales = sb("mv_scales%d" % b, [P, P], U8)
+        mv_codes = []
+        mv_scales = []
+        for h in range(2):
+            grouped = sb("mv_grouped%d" % h, [P, E // 2, PACK], BF16)
+            if h == 0:
+                nc.scalar.copy(
+                    grouped[:].rearrange("p (c i) j -> p c j i", i=4),
+                    mv_raw[h][:].rearrange("p j (c i) -> p c j i", i=4),
+                )
+            else:
+                nc.gpsimd.tensor_scalar(grouped[:], mv_raw[h][:].rearrange("p j e -> p e j"), 1.0, 0.0, ALU.mult, ALU.add)
+            codes = sb("mv_codes%d" % h, [P, E // 2], U32, tag="late_a" if h == 0 else "late_b")
+            scales = sb("mv_scales%d" % h, [P, E // 2], U8)
             nc.vector.quantize_mx(out=codes[:].bitcast(FP8X4), scales=scales[:], in_=grouped[:].rearrange("p e j -> p (e j)"))
-            mv_codes[b] = codes[:]
-            mv_scales[b] = scales[:]
+            for b in range(2):
+                mv_codes.append(codes[:, b * P : (b + 1) * P])
+                mv_scales.append(scales[:, b * P : (b + 1) * P])
 
         out_rows = out.rearrange("(b p) i -> p b i", p=P)
-        for c in range(CHUNKS):
-            cols = slice(c * CHUNK, (c + 1) * CHUNK)
-            w = sb("w%d" % c, [P, CHUNK, PACK], BF16)
+        pieces = [(0, 0, 128), (1, 0, 128), (2, 0, 128), (3, 0, 128)]
+        for n, (c, first, width) in enumerate(pieces):
+            in_half = (c % 2) * CHUNK + first
+            cols = slice(c * CHUNK + first, c * CHUNK + first + width)
+            w = sb("w%d" % n, [P, width, PACK], BF16)
             nc.vector.tensor_tensor(
                 w[:].rearrange("p (g i) r -> p g r i", i=4),
-                scaled[:, :, cols].rearrange("p r (g i) -> p g r i", i=4),
-                spread[c][:].rearrange("p (g i) -> p g i", i=4).unsqueeze(2).to_broadcast([P, CHUNK // 4, PACK, 4]),
+                scaled[c // 2][:, :, in_half : in_half + width].rearrange("p r (g i) -> p g r i", i=4),
+                spread[c][:, first : first + width].rearrange("p (g i) -> p g i", i=4).unsqueeze(2).to_broadcast([P, width // 4, PACK, 4]),
                 ALU.mult,
             )
-            w_codes = sb("w_codes%d" % c, [P, CHUNK], U32)
-            w_scales = sb("w_scales%d" % c, [P, CHUNK], U8)
+            w_codes = sb("w_codes%d" % n, [P, width], U32)
+            w_scales = sb("w_scales%d" % n, [P, width], U8)
             nc.vector.quantize_mx(out=w_codes[:].bitcast(FP8X4), scales=w_scales[:], in_=w[:].rearrange("p i r -> p (i r)"))
-            parts = [(0, 4, 4 + c)] if c < CHUNKS - 1 else [(0, 2, 4 + c), (2, 4, 0)]
+            parts = [(0, 4, 4 + c)] if n < len(pieces) - 1 else [(0, 2, 7), (2, 4, 0)]
             for k, (b0, b1, bk) in enumerate(parts):
-                acc = bank("acc%d_%d" % (c, k), [P, b1 - b0, CHUNK], bk)
+                acc = bank("acc%d_%d" % (n, k), [P, b1 - b0, width], bk)
                 for b in range(b0, b1):
                     nc.tensor.matmul_mx(
                         out=acc[:, b - b0, :],
@@ -193,9 +221,10 @@ def tile_attend_externalattn_kernel(tc, tok_words, tok_scales, mk, msc, mv, offs
                         start=True,
                         stop=True,
                     )
-                result = sb("result%d_%d" % (c, k), [P, b1 - b0, CHUNK], F32)
+                result = sb("result%d_%d" % (n, k), [P, b1 - b0, width], F32)
                 if k == 0:
                     nc.scalar.copy(result[:], acc[:])
                 else:
                     nc.vector.tensor_copy(result[:], acc[:])
-                nc.sync.dma_start(out_rows[:, b0:b1, cols], result[:])
+                queue = nc.scalar if (n, k) == (len(pieces) - 1, 0) else nc.sync
+                queue.dma_start(out_rows[:, b0:b1, cols], result[:])

@@ -44,8 +44,8 @@ def tile_attend_externalattn_kernel(tc, tok_words, tok_scales, mk, msc, mv, offs
         nc.gpsimd.memset(pool_scales[:].bitcast(I32), 0)
         for q in range(4):
             nc.sync.dma_start(
-                pool_scales[32 * q : 32 * q + 4, :].bitcast(I32),
-                tok_scales[0, 4 * q : 4 * q + 4, :].bitcast(I32),
+                pool_scales[q:P:32, :].bitcast(I32),
+                tok_scales[0, q:16:4, :].bitcast(I32),
             )
         mk_rows = mk.rearrange("(p j) m -> p j m", j=PACK)
         mk_raw = []
@@ -194,37 +194,35 @@ def tile_attend_externalattn_kernel(tc, tok_words, tok_scales, mk, msc, mv, offs
                 mv_scales.append(scales[:, b * P : (b + 1) * P])
 
         out_rows = out.rearrange("(b p) i -> p b i", p=P)
-        pieces = [(0, 0, 128), (1, 0, 128), (2, 0, 128), (3, 0, 128)]
-        for n, (c, first, width) in enumerate(pieces):
-            in_half = (c % 2) * CHUNK + first
-            cols = slice(c * CHUNK + first, c * CHUNK + first + width)
-            w = sb("w%d" % n, [P, width, PACK], BF16)
-            nc.vector.tensor_tensor(
-                w[:].rearrange("p (g i) r -> p g r i", i=4),
-                scaled[c // 2][:, :, in_half : in_half + width].rearrange("p r (g i) -> p g r i", i=4),
-                spread[c][:, first : first + width].rearrange("p (g i) -> p g i", i=4).unsqueeze(2).to_broadcast([P, width // 4, PACK, 4]),
-                ALU.mult,
-            )
-            w_codes = sb("w_codes%d" % n, [P, width], U32)
-            w_scales = sb("w_scales%d" % n, [P, width], U8)
+        for c in range(CHUNKS):
+            cols = slice(c * CHUNK, (c + 1) * CHUNK)
+            w = sb("w%d" % c, [P, CHUNK, PACK], BF16)
+            for first, width in [(0, 128)] if c == 0 else [(0, 64), (64, 64)]:
+                in_half = (c % 2) * CHUNK + first
+                nc.vector.tensor_tensor(
+                    w[:, first : first + width].rearrange("p (g i) r -> p g r i", i=4),
+                    scaled[c // 2][:, :, in_half : in_half + width].rearrange("p r (g i) -> p g r i", i=4),
+                    spread[c][:, first : first + width].rearrange("p (g i) -> p g i", i=4).unsqueeze(2).to_broadcast([P, width // 4, PACK, 4]),
+                    ALU.mult,
+                )
+            w_codes = sb("w_codes%d" % c, [P, CHUNK], U32)
+            w_scales = sb("w_scales%d" % c, [P, CHUNK], U8)
             nc.vector.quantize_mx(out=w_codes[:].bitcast(FP8X4), scales=w_scales[:], in_=w[:].rearrange("p i r -> p (i r)"))
-            parts = [(0, 4, 4 + c)] if n < len(pieces) - 1 else [(0, 2, 7), (2, 4, 0)]
-            for k, (b0, b1, bk) in enumerate(parts):
-                acc = bank("acc%d_%d" % (n, k), [P, b1 - b0, width], bk)
-                for b in range(b0, b1):
+            for k in range(2):
+                acc = bank("acc%d_%d" % (c, k), [P, 2, CHUNK], 4 + c if k == 0 else c)
+                for b in range(2):
                     nc.tensor.matmul_mx(
-                        out=acc[:, b - b0, :],
-                        lhsT=mv_codes[b].bitcast(FP8X4),
-                        lhsT_scale=mv_scales[b],
+                        out=acc[:, b, :],
+                        lhsT=mv_codes[2 * k + b].bitcast(FP8X4),
+                        lhsT_scale=mv_scales[2 * k + b],
                         rhs=w_codes[:].bitcast(FP8X4),
                         rhs_scale=w_scales[:],
                         start=True,
                         stop=True,
                     )
-                result = sb("result%d_%d" % (n, k), [P, b1 - b0, width], F32)
-                if k == 0:
-                    nc.scalar.copy(result[:], acc[:])
-                else:
+                result = sb("result%d_%d" % (c, k), [P, 2, CHUNK], F32)
+                if (c, k) == (CHUNKS - 1, 1):
                     nc.vector.tensor_copy(result[:], acc[:])
-                queue = nc.scalar if (n, k) == (len(pieces) - 1, 0) else nc.sync
-                queue.dma_start(out_rows[:, b0:b1, cols], result[:])
+                else:
+                    nc.scalar.copy(result[:], acc[:])
+                nc.sync.dma_start(out_rows[:, 2 * k : 2 * k + 2, cols], result[:])

@@ -20,8 +20,14 @@ AX = mybir.AxisListType
 
 P = 128
 PACK = 4
+LIST_GROUP = 16
+QUADRANT = 32
+SCALE_ROWS = D // 32
+HALF = 256
 CHUNK = 128
 CHUNKS = I // CHUNK
+RUN = 4
+TURNED_BANK = PACK
 
 
 def tile_attend_externalattn_kernel(tc, tok_words, tok_scales, mk, msc, mv, offs, out):
@@ -30,72 +36,73 @@ def tile_attend_externalattn_kernel(tc, tok_words, tok_scales, mk, msc, mv, offs
         keep = ctx.enter_context(tc.tile_pool(name="keep", bufs=1))
         psum = ctx.enter_context(tc.psum_pool(name="psum", bufs=1))
 
-        def sb(name, shape, dtype, tag=None):
+        def sbuf(name, shape, dtype, tag=None):
             return keep.tile(shape, dtype, name=name, tag=tag or name, align_bytes=64)
 
-        def bank(name, shape, k):
-            return psum.tile(shape, F32, name=name, tag="bank%d" % k)
+        def bank(name, shape, number):
+            return psum.tile(shape, F32, name=name, tag="bank%d" % number)
 
-        offsets = keep.tile([P, I // 16], U16, name="offsets")
+        offsets = keep.tile([P, I // LIST_GROUP], U16, name="offsets")
         nc.sync.dma_start(offsets[:], offs)
-        pool_words = sb("pool_words", [P, T], U16)
+        pool_words = sbuf("pool_words", [P, T], U16)
         nc.sync.dma_start(pool_words[:].bitcast(I32), tok_words[0].bitcast(I32))
-        pool_scales = sb("pool_scales", [P, T], U8)
+        pool_scales = sbuf("pool_scales", [P, T], U8)
         nc.gpsimd.memset(pool_scales[:].bitcast(I32), 0)
-        for q in range(4):
+        for f in range(4):
             nc.sync.dma_start(
-                pool_scales[q:P:32, :].bitcast(I32),
-                tok_scales[0, q:16:4, :].bitcast(I32),
+                pool_scales[f:P:QUADRANT, :].bitcast(I32),
+                tok_scales[0, f:SCALE_ROWS:4, :].bitcast(I32),
             )
-        mk_rows = mk.rearrange("(p j) m -> p j m", j=PACK)
+        mk_rows = mk.rearrange("(p t) m -> p t m", t=PACK)
         mk_raw = []
-        for h in range(2):
-            raw = sb("mk_raw%d" % h, [P, PACK, M // 2], F32)
-            nc.sync.dma_start(raw[:], mk_rows[:, :, h * 256 : (h + 1) * 256])
+        for half in range(2):
+            raw = sbuf("mk_raw%d" % half, [P, PACK, HALF], F32)
+            nc.sync.dma_start(raw[:], mk_rows[:, :, half * HALF : (half + 1) * HALF])
             mk_raw.append(raw)
-        mv_rows = mv.rearrange("(p j) e -> p j e", j=PACK)
+        mv_rows = mv.rearrange("(p t) e -> p t e", t=PACK)
         mv_raw = []
-        for h in range(2):
-            raw = sb("mv_raw%d" % h, [P, PACK, E // 2], F32)
-            nc.sync.dma_start(raw[:], mv_rows[:, :, h * 256 : (h + 1) * 256])
+        for half in range(2):
+            raw = sbuf("mv_raw%d" % half, [P, PACK, HALF], F32)
+            nc.sync.dma_start(raw[:], mv_rows[:, :, half * HALF : (half + 1) * HALF])
             mv_raw.append(raw)
-        msc_sb = sb("msc_sb", [P, PACK], F32)
-        nc.sync.dma_start(msc_sb[:], msc.rearrange("(p r) o -> p (r o)", r=PACK))
+        key_scale = sbuf("key_scale", [P, PACK], F32)
+        nc.sync.dma_start(key_scale[:], msc.rearrange("(p r) o -> p (r o)", r=PACK))
 
-        ident = sb("ident", [P, P], F32)
-        make_identity(nc, ident[:])
-        warm = sb("warm", [P, 1], F32)
-        nc.scalar.activation(warm[:], ident[:, 0:1], ACT.Exp)
+        identity = sbuf("identity", [P, P], F32)
+        make_identity(nc, identity[:])
+        table_preload = sbuf("table_preload", [P, 1], F32)
+        nc.scalar.activation(table_preload[:], identity[:, 0:1], ACT.Exp)
 
-        tok_w = sb("tok_w", [P, I], U16)
-        nc.vector.tensor_copy(tok_w[:], pool_words[:].indirect(offsets[:]))
-        tok_s = sb("tok_s", [P, I], U8)
-        nc.vector.tensor_copy(tok_s[:], pool_scales[:].indirect(offsets[:]))
+        token_words = sbuf("token_words", [P, I], U16)
+        nc.vector.tensor_copy(token_words[:], pool_words[:].indirect(offsets[:]))
+        token_scales = sbuf("token_scales", [P, I], U8)
+        nc.vector.tensor_copy(token_scales[:], pool_scales[:].indirect(offsets[:]))
 
-        mk_codes = [sb("mk_codes%d" % r, [P, P], U32) for r in range(PACK)]
-        mk_scales = [sb("mk_scales%d" % r, [P, P], U8) for r in range(PACK)]
+        mk_codes = [sbuf("mk_codes%d" % r, [P, P], U32) for r in range(PACK)]
+        mk_scales = [sbuf("mk_scales%d" % r, [P, P], U8) for r in range(PACK)]
+        dealt_half = HALF // PACK
         for pair in range(2):
-            grouped = sb("mk_grouped%d" % pair, [P, 2, P, PACK], BF16)
-            for h in range(2):
-                by_place = mk_raw[h][:].rearrange("p j (s r) -> p s j r", r=PACK)
-                dst = grouped[:, :, 64 * h : 64 * h + 64, :].rearrange("p r s j -> p s j r")
-                src = by_place[:, :, :, 2 * pair : 2 * pair + 2]
-                if (pair, h) == (0, 1):
-                    nc.vector.tensor_copy(dst, src)
+            mk_grouped = sbuf("mk_grouped%d" % pair, [P, 2, P, PACK], BF16)
+            for half in range(2):
+                by_operand = mk_raw[half][:].rearrange("p t (c r) -> p c t r", r=PACK)
+                target = mk_grouped[:, :, dealt_half * half : dealt_half * (half + 1), :].rearrange("p r c t -> p c t r")
+                source = by_operand[:, :, :, 2 * pair : 2 * pair + 2]
+                if pair == 0 and half == 1:
+                    nc.vector.tensor_copy(target, source)
                 else:
-                    nc.scalar.copy(dst, src)
-            for rr in range(2):
-                r = 2 * pair + rr
+                    nc.scalar.copy(target, source)
+            for in_pair in range(2):
+                r = 2 * pair + in_pair
                 nc.vector.quantize_mx(
                     out=mk_codes[r][:].bitcast(FP8X4),
                     scales=mk_scales[r][:],
-                    in_=grouped[:, rr].rearrange("p s j -> p (s j)"),
+                    in_=mk_grouped[:, in_pair].rearrange("p c t -> p (c t)"),
                 )
 
-        p_sb = [sb("p%d" % r, [P, I], F32) for r in range(PACK)]
-        row_sum01 = sb("row_sum01", [P, 2], F32)
-        row_sum2 = sb("row_sum2", [P, 1], F32)
-        row_sum3 = sb("row_sum3", [P, 1], F32, tag="late_b")
+        exps = [sbuf("exps%d" % r, [P, I], F32) for r in range(PACK)]
+        row_sum01 = sbuf("row_sum01", [P, 2], F32)
+        row_sum2 = sbuf("row_sum2", [P, 1], F32)
+        row_sum3 = sbuf("row_sum3", [P, 1], F32, tag="last_row_sum")
         row_sum = [row_sum01[:, 0:1], row_sum01[:, 1:2], row_sum2[:], row_sum3[:]]
         for r in range(PACK):
             scores = bank("scores%d" % r, [P, I], r)
@@ -103,126 +110,146 @@ def tile_attend_externalattn_kernel(tc, tok_words, tok_scales, mk, msc, mv, offs
                 out=scores[:],
                 lhsT=mk_codes[r][:].bitcast(FP8X4),
                 lhsT_scale=mk_scales[r][:],
-                rhs=tok_w[:].bitcast(FP4X4),
-                rhs_scale=tok_s[:],
+                rhs=token_words[:].bitcast(FP4X4),
+                rhs_scale=token_scales[:],
                 start=True,
                 stop=True,
             )
-            last = r == PACK - 1
-            neg_max = sb("neg_max%d" % r, [P, 1], F32, tag="late_a" if last else None)
+            neg_max = sbuf("neg_max%d" % r, [P, 1], F32, tag="last_row_max" if r == PACK - 1 else None)
             nc.vector.tensor_reduce(neg_max[:], scores[:], AX.X, ALU.max, negate=True)
-            nc.scalar.activation(
-                p_sb[r][:], scores[:], ACT.Exp, bias=neg_max[:], scale=1.0,
-                accum_out=row_sum[r],
-            )
+            nc.scalar.activation(exps[r][:], scores[:], ACT.Exp, bias=neg_max[:], scale=1.0, accum_out=row_sum[r])
 
-        row_inv = sb("row_inv", [P, PACK], F32)
-        factor = sb("factor", [P, PACK], F32)
-        inv = [row_inv[:, r : r + 1] for r in range(PACK)]
-        fac = [factor[:, r : r + 1] for r in range(PACK)]
+        row_inv = sbuf("row_inv", [P, PACK], F32)
+        factor = sbuf("factor", [P, PACK], F32)
         shares = {}
 
-        def share(r, c0, c1):
-            t = sb("share%d_%d" % (r, c0), [P, (c1 - c0) * CHUNK], F32)
-            nc.vector.tensor_scalar(t[:], p_sb[r][:, c0 * CHUNK : c1 * CHUNK], inv[r], None, ALU.mult)
-            for c in range(c0, c1):
-                shares[(r, c)] = t[:, (c - c0) * CHUNK : (c - c0 + 1) * CHUNK]
+        def make_shares(r, first_chunk, end_chunk):
+            part = sbuf("shares%d_%d" % (r, first_chunk), [P, (end_chunk - first_chunk) * CHUNK], F32)
+            slots = slice(first_chunk * CHUNK, end_chunk * CHUNK)
+            nc.vector.tensor_scalar(part[:], exps[r][:, slots], row_inv[:, r : r + 1], None, ALU.mult)
+            for chunk in range(first_chunk, end_chunk):
+                shares[(r, chunk)] = part[:, (chunk - first_chunk) * CHUNK : (chunk - first_chunk + 1) * CHUNK]
 
         nc.vector.reciprocal(row_inv[:, 0:2], row_sum01[:])
-        nc.vector.tensor_tensor(factor[:, 0:2], row_inv[:, 0:2], msc_sb[:, 0:2], ALU.mult)
-        nc.vector.reciprocal(inv[2], row_sum[2])
-        nc.vector.reciprocal(inv[3], row_sum[3])
-        share(3, 0, 1)
-        share(2, 0, 1)
-        share(0, 0, 4)
-        share(1, 0, 4)
-        nc.vector.tensor_tensor(factor[:, 2:4], row_inv[:, 2:4], msc_sb[:, 2:4], ALU.mult)
-        share(2, 1, 4)
-        share(3, 1, 4)
+        nc.vector.tensor_tensor(factor[:, 0:2], row_inv[:, 0:2], key_scale[:, 0:2], ALU.mult)
+        nc.vector.reciprocal(row_inv[:, 2:3], row_sum[2])
+        nc.vector.reciprocal(row_inv[:, 3:4], row_sum[3])
+        make_shares(3, 0, 1)
+        make_shares(2, 0, 1)
+        make_shares(0, 0, CHUNKS)
+        make_shares(1, 0, CHUNKS)
+        nc.vector.tensor_tensor(factor[:, 2:4], row_inv[:, 2:4], key_scale[:, 2:4], ALU.mult)
+        make_shares(2, 1, CHUNKS)
+        make_shares(3, 1, CHUNKS)
 
-        scaled = [sb("scaled%d" % h, [P, PACK, I // 2], F32) for h in range(2)]
+        scaled = [sbuf("scaled%d" % half, [P, PACK, HALF], F32) for half in range(2)]
 
-        def scale_half(h):
+        def scale_half(half):
             for r in range(PACK):
-                nc.scalar.activation(scaled[h][:, r, :], p_sb[r][:, h * 256 : (h + 1) * 256], ACT.Copy, scale=fac[r])
+                slots = slice(half * HALF, (half + 1) * HALF)
+                nc.scalar.activation(scaled[half][:, r, :], exps[r][:, slots], ACT.Copy, scale=factor[:, r : r + 1])
 
         scale_half(0)
 
+        warm_up = bank("warm_up", [P, I], 1)
+        for repeat in range(2):
+            nc.tensor.matmul_mx(
+                out=warm_up[:],
+                lhsT=mk_codes[0][:].bitcast(FP8X4),
+                lhsT_scale=mk_scales[0][:],
+                rhs=token_words[:].bitcast(FP4X4),
+                rhs_scale=token_scales[:],
+                start=(repeat == 0),
+                stop=(repeat == 1),
+            )
+
         turned = []
-        for c in range(CHUNKS):
-            t = bank("turned%d" % c, [P, P], 4 + c)
+        for chunk in range(CHUNKS):
+            turned_bank = bank("turned%d" % chunk, [P, P], TURNED_BANK + chunk)
             for r in range(PACK):
-                nc.tensor.matmul(t[:], shares[(r, c)], ident[:], start=(r == 0), stop=(r == PACK - 1), is_transpose=True)
-            turned.append(t)
+                nc.tensor.matmul(
+                    turned_bank[:], shares[(r, chunk)], identity[:],
+                    start=(r == 0), stop=(r == PACK - 1), is_transpose=True,
+                )
+            turned.append(turned_bank)
         col_inv = []
-        for c in range(2):
-            col_sum = sb("col_sum%d" % c, [P, 1], F32)
-            nc.vector.tensor_reduce(col_sum[:], turned[c][:], AX.X, ALU.add)
-            one = sb("col_inv%d" % c, [P, 1], F32)
-            nc.vector.reciprocal(one[:], col_sum[:])
-            col_inv.append(one[:])
-        col_sum23 = sb("col_sum23", [P, 2], F32)
-        for c in range(2, 4):
-            spent = sb("spent%d" % c, [P, P], F32)
-            nc.scalar.activation(spent[:], turned[c][:], ACT.Copy, accum_out=col_sum23[:, c - 2 : c - 1])
-        col_inv23 = sb("col_inv23", [P, 2], F32)
+        for chunk in range(2):
+            col_sum = sbuf("col_sum%d" % chunk, [P, 1], F32)
+            nc.vector.tensor_reduce(col_sum[:], turned[chunk][:], AX.X, ALU.add)
+            inverse = sbuf("col_inv%d" % chunk, [P, 1], F32)
+            nc.vector.reciprocal(inverse[:], col_sum[:])
+            col_inv.append(inverse[:])
+        col_sum23 = sbuf("col_sum23", [P, 2], F32)
+        for chunk in range(2, CHUNKS):
+            by_product = sbuf("by_product%d" % chunk, [P, P], F32)
+            nc.scalar.activation(by_product[:], turned[chunk][:], ACT.Copy, accum_out=col_sum23[:, chunk - 2 : chunk - 1])
+        col_inv23 = sbuf("col_inv23", [P, 2], F32)
         nc.vector.reciprocal(col_inv23[:], col_sum23[:])
         col_inv.extend([col_inv23[:, 0:1], col_inv23[:, 1:2]])
         spread = []
-        for c in range(CHUNKS):
-            wide = bank("spread%d" % c, [P, CHUNK], c)
-            nc.tensor.transpose(wide[:], col_inv[c].to_broadcast([P, P]), ident[:])
-            spread.append(wide)
+        for chunk in range(CHUNKS):
+            spread_bank = bank("spread%d" % chunk, [P, CHUNK], chunk)
+            nc.tensor.transpose(spread_bank[:], col_inv[chunk].to_broadcast([P, P]), identity[:])
+            spread.append(spread_bank)
         scale_half(1)
 
         mv_codes = []
         mv_scales = []
-        for h in range(2):
-            grouped = sb("mv_grouped%d" % h, [P, E // 2, PACK], BF16)
-            if h == 0:
+        for half in range(2):
+            mv_grouped = sbuf("mv_grouped%d" % half, [P, HALF, PACK], BF16)
+            if half == 0:
                 nc.scalar.copy(
-                    grouped[:].rearrange("p (c i) j -> p c j i", i=4),
-                    mv_raw[h][:].rearrange("p j (c i) -> p c j i", i=4),
+                    mv_grouped[:].rearrange("p (g n) t -> p g t n", n=RUN),
+                    mv_raw[half][:].rearrange("p t (g n) -> p g t n", n=RUN),
                 )
             else:
-                nc.gpsimd.tensor_scalar(grouped[:], mv_raw[h][:].rearrange("p j e -> p e j"), 1.0, 0.0, ALU.mult, ALU.add)
-            codes = sb("mv_codes%d" % h, [P, E // 2], U32, tag="late_a" if h == 0 else "late_b")
-            scales = sb("mv_scales%d" % h, [P, E // 2], U8)
-            nc.vector.quantize_mx(out=codes[:].bitcast(FP8X4), scales=scales[:], in_=grouped[:].rearrange("p e j -> p (e j)"))
-            for b in range(2):
-                mv_codes.append(codes[:, b * P : (b + 1) * P])
-                mv_scales.append(scales[:, b * P : (b + 1) * P])
+                nc.gpsimd.tensor_scalar(
+                    mv_grouped[:], mv_raw[half][:].rearrange("p t e -> p e t"), 1.0, 0.0, ALU.mult, ALU.add
+                )
+            codes = sbuf("mv_codes%d" % half, [P, HALF], U32, tag="last_row_max" if half == 0 else "last_row_sum")
+            scales = sbuf("mv_scales%d" % half, [P, HALF], U8)
+            nc.vector.quantize_mx(
+                out=codes[:].bitcast(FP8X4), scales=scales[:], in_=mv_grouped[:].rearrange("p e t -> p (e t)")
+            )
+            for first in range(0, HALF, P):
+                mv_codes.append(codes[:, first : first + P])
+                mv_scales.append(scales[:, first : first + P])
 
         out_rows = out.rearrange("(b p) i -> p b i", p=P)
-        for c in range(CHUNKS):
-            cols = slice(c * CHUNK, (c + 1) * CHUNK)
-            w = sb("w%d" % c, [P, CHUNK, PACK], BF16)
-            for first, width in [(0, 128)] if c == 0 else [(0, 64), (64, 64)]:
-                in_half = (c % 2) * CHUNK + first
+        for chunk in range(CHUNKS):
+            slots = slice(chunk * CHUNK, (chunk + 1) * CHUNK)
+            weights = sbuf("weights%d" % chunk, [P, CHUNK, PACK], BF16)
+            width = CHUNK if chunk == 0 else CHUNK // 2
+            for first in range(0, CHUNK, width):
+                in_half = (chunk % 2) * CHUNK + first
+                inverse_sums = spread[chunk][:, first : first + width].rearrange("p (g n) -> p g n", n=RUN)
                 nc.vector.tensor_tensor(
-                    w[:, first : first + width].rearrange("p (g i) r -> p g r i", i=4),
-                    scaled[c // 2][:, :, in_half : in_half + width].rearrange("p r (g i) -> p g r i", i=4),
-                    spread[c][:, first : first + width].rearrange("p (g i) -> p g i", i=4).unsqueeze(2).to_broadcast([P, width // 4, PACK, 4]),
+                    weights[:, first : first + width].rearrange("p (g n) r -> p g r n", n=RUN),
+                    scaled[chunk // 2][:, :, in_half : in_half + width].rearrange("p r (g n) -> p g r n", n=RUN),
+                    inverse_sums.unsqueeze(2).to_broadcast([P, width // RUN, PACK, RUN]),
                     ALU.mult,
                 )
-            w_codes = sb("w_codes%d" % c, [P, CHUNK], U32)
-            w_scales = sb("w_scales%d" % c, [P, CHUNK], U8)
-            nc.vector.quantize_mx(out=w_codes[:].bitcast(FP8X4), scales=w_scales[:], in_=w[:].rearrange("p i r -> p (i r)"))
-            for k in range(2):
-                acc = bank("acc%d_%d" % (c, k), [P, 2, CHUNK], 4 + c if k == 0 else c)
-                for b in range(2):
+            w_codes = sbuf("w_codes%d" % chunk, [P, CHUNK], U32)
+            w_scales = sbuf("w_scales%d" % chunk, [P, CHUNK], U8)
+            nc.vector.quantize_mx(
+                out=w_codes[:].bitcast(FP8X4), scales=w_scales[:], in_=weights[:].rearrange("p i r -> p (i r)")
+            )
+            for side in range(2):
+                sums = bank("sums%d_%d" % (chunk, side), [P, 2, CHUNK], TURNED_BANK + chunk if side == 0 else chunk)
+                for in_bank in range(2):
+                    group = 2 * side + in_bank
                     nc.tensor.matmul_mx(
-                        out=acc[:, b, :],
-                        lhsT=mv_codes[2 * k + b].bitcast(FP8X4),
-                        lhsT_scale=mv_scales[2 * k + b],
+                        out=sums[:, in_bank, :],
+                        lhsT=mv_codes[group].bitcast(FP8X4),
+                        lhsT_scale=mv_scales[group],
                         rhs=w_codes[:].bitcast(FP8X4),
                         rhs_scale=w_scales[:],
                         start=True,
                         stop=True,
                     )
-                result = sb("result%d_%d" % (c, k), [P, 2, CHUNK], F32)
-                if (c, k) == (CHUNKS - 1, 1):
-                    nc.vector.tensor_copy(result[:], acc[:])
+                result = sbuf("result%d_%d" % (chunk, side), [P, 2, CHUNK], F32)
+                if chunk == CHUNKS - 1 and side == 1:
+                    nc.vector.tensor_copy(result[:], sums[:])
                 else:
-                    nc.scalar.copy(result[:], acc[:])
-                nc.sync.dma_start(out_rows[:, 2 * k : 2 * k + 2, cols], result[:])
+                    nc.scalar.copy(result[:], sums[:])
+                nc.sync.dma_start(out_rows[:, 2 * side : 2 * side + 2, slots], result[:])

@@ -27,6 +27,8 @@ HALF = 256
 CHUNK = 128
 CHUNKS = I // CHUNK
 RUN = 4
+MK_PIECES = ((0, 256), (256, 384), (384, 512))
+GROUPS = E // P
 TURNED_BANK = PACK
 
 
@@ -42,10 +44,10 @@ def tile_attend_externalattn_kernel(tc, tok_words, tok_scales, mk, msc, mv, offs
         def bank(name, shape, number):
             return psum.tile(shape, F32, name=name, tag="bank%d" % number)
 
-        offsets = keep.tile([P, I // LIST_GROUP], U16, name="offsets")
-        nc.sync.dma_start(offsets[:], offs)
         pool_words = sbuf("pool_words", [P, T], U16)
         nc.sync.dma_start(pool_words[:].bitcast(I32), tok_words[0].bitcast(I32))
+        offsets = keep.tile([P, I // LIST_GROUP], U16, name="offsets")
+        nc.sync.dma_start(offsets[:], offs)
         pool_scales = sbuf("pool_scales", [P, T], U8)
         nc.gpsimd.memset(pool_scales[:].bitcast(I32), 0)
         for f in range(4):
@@ -55,15 +57,15 @@ def tile_attend_externalattn_kernel(tc, tok_words, tok_scales, mk, msc, mv, offs
             )
         mk_rows = mk.rearrange("(p t) m -> p t m", t=PACK)
         mk_raw = []
-        for half in range(2):
-            raw = sbuf("mk_raw%d" % half, [P, PACK, HALF], F32)
-            nc.sync.dma_start(raw[:], mk_rows[:, :, half * HALF : (half + 1) * HALF])
+        for piece, (first, end) in enumerate(MK_PIECES):
+            raw = sbuf("mk_raw%d" % piece, [P, PACK, end - first], F32)
+            nc.sync.dma_start(raw[:], mk_rows[:, :, first:end])
             mk_raw.append(raw)
         mv_rows = mv.rearrange("(p t) e -> p t e", t=PACK)
         mv_raw = []
-        for half in range(2):
-            raw = sbuf("mv_raw%d" % half, [P, PACK, HALF], F32)
-            nc.sync.dma_start(raw[:], mv_rows[:, :, half * HALF : (half + 1) * HALF])
+        for group in range(GROUPS):
+            raw = sbuf("mv_raw%d" % group, [P, PACK, P], F32)
+            nc.sync.dma_start(raw[:], mv_rows[:, :, group * P : (group + 1) * P])
             mv_raw.append(raw)
         key_scale = sbuf("key_scale", [P, PACK], F32)
         nc.sync.dma_start(key_scale[:], msc.rearrange("(p r) o -> p (r o)", r=PACK))
@@ -80,30 +82,53 @@ def tile_attend_externalattn_kernel(tc, tok_words, tok_scales, mk, msc, mv, offs
 
         mk_codes = [sbuf("mk_codes%d" % r, [P, P], U32) for r in range(PACK)]
         mk_scales = [sbuf("mk_scales%d" % r, [P, P], U8) for r in range(PACK)]
-        dealt_half = HALF // PACK
+        mk_grouped = [sbuf("mk_grouped%d" % pair, [P, 2, P, PACK], BF16) for pair in range(2)]
         for pair in range(2):
-            mk_grouped = sbuf("mk_grouped%d" % pair, [P, 2, P, PACK], BF16)
-            for half in range(2):
-                by_operand = mk_raw[half][:].rearrange("p t (c r) -> p c t r", r=PACK)
-                target = mk_grouped[:, :, dealt_half * half : dealt_half * (half + 1), :].rearrange("p r c t -> p c t r")
+            for piece, (first, end) in enumerate(MK_PIECES):
+                by_operand = mk_raw[piece][:].rearrange("p t (c r) -> p c t r", r=PACK)
+                target = mk_grouped[pair][:, :, first // PACK : end // PACK, :].rearrange("p r c t -> p c t r")
                 source = by_operand[:, :, :, 2 * pair : 2 * pair + 2]
-                if pair == 0 and half == 1:
-                    nc.vector.tensor_copy(target, source)
-                else:
+                if piece == 0 or (piece == 1 and pair == 0) or (piece == 2 and pair == 1):
                     nc.scalar.copy(target, source)
+                else:
+                    nc.vector.tensor_copy(target, source)
             for in_pair in range(2):
-                r = 2 * pair + in_pair
                 nc.vector.quantize_mx(
-                    out=mk_codes[r][:].bitcast(FP8X4),
-                    scales=mk_scales[r][:],
-                    in_=mk_grouped[:, in_pair].rearrange("p c t -> p (c t)"),
+                    out=mk_codes[2 * pair + in_pair][:].bitcast(FP8X4),
+                    scales=mk_scales[2 * pair + in_pair][:],
+                    in_=mk_grouped[pair][:, in_pair].rearrange("p c t -> p (c t)"),
                 )
+
+        mv_grouped = []
+        for group in range(GROUPS):
+            grouped = sbuf("mv_grouped%d" % group, [P, P, PACK], BF16)
+            if group < 2:
+                nc.scalar.copy(
+                    grouped[:].rearrange("p (g n) t -> p g t n", n=RUN),
+                    mv_raw[group][:].rearrange("p t (g n) -> p g t n", n=RUN),
+                )
+            else:
+                nc.gpsimd.tensor_scalar(
+                    grouped[:], mv_raw[group][:].rearrange("p t e -> p e t"), 1.0, 0.0, ALU.mult, ALU.add
+                )
+            mv_grouped.append(grouped)
+
+        mv_codes = []
+        mv_scales = []
+
+        def quantise_mv(group):
+            codes = sbuf("mv_codes%d" % group, [P, P], U32, tag=("row_max1", "row_max3", "row_sum23", "col_sum0")[group])
+            scales = sbuf("mv_scales%d" % group, [P, P], U8)
+            nc.vector.quantize_mx(
+                out=codes[:].bitcast(FP8X4), scales=scales[:], in_=mv_grouped[group][:].rearrange("p e t -> p (e t)")
+            )
+            mv_codes.append(codes[:])
+            mv_scales.append(scales[:])
 
         exps = [sbuf("exps%d" % r, [P, I], F32) for r in range(PACK)]
         row_sum01 = sbuf("row_sum01", [P, 2], F32)
-        row_sum2 = sbuf("row_sum2", [P, 1], F32)
-        row_sum3 = sbuf("row_sum3", [P, 1], F32, tag="last_row_sum")
-        row_sum = [row_sum01[:, 0:1], row_sum01[:, 1:2], row_sum2[:], row_sum3[:]]
+        row_sum23 = sbuf("row_sum23", [P, 2], F32)
+        row_sum = [row_sum01[:, 0:1], row_sum01[:, 1:2], row_sum23[:, 0:1], row_sum23[:, 1:2]]
         for r in range(PACK):
             scores = bank("scores%d" % r, [P, I], r)
             nc.tensor.matmul_mx(
@@ -115,41 +140,40 @@ def tile_attend_externalattn_kernel(tc, tok_words, tok_scales, mk, msc, mv, offs
                 start=True,
                 stop=True,
             )
-            neg_max = sbuf("neg_max%d" % r, [P, 1], F32, tag="last_row_max" if r == PACK - 1 else None)
+            neg_max = sbuf("neg_max%d" % r, [P, 1], F32, tag="row_max%d" % r)
             nc.vector.tensor_reduce(neg_max[:], scores[:], AX.X, ALU.max, negate=True)
             nc.scalar.activation(exps[r][:], scores[:], ACT.Exp, bias=neg_max[:], scale=1.0, accum_out=row_sum[r])
 
         row_inv = sbuf("row_inv", [P, PACK], F32)
-        factor = sbuf("factor", [P, PACK], F32)
-        shares = {}
+        shares = [sbuf("shares%d" % r, [P, I], F32) for r in range(PACK)]
 
-        def make_shares(r, first_chunk, end_chunk):
-            part = sbuf("shares%d_%d" % (r, first_chunk), [P, (end_chunk - first_chunk) * CHUNK], F32)
-            slots = slice(first_chunk * CHUNK, end_chunk * CHUNK)
-            nc.vector.tensor_scalar(part[:], exps[r][:, slots], row_inv[:, r : r + 1], None, ALU.mult)
-            for chunk in range(first_chunk, end_chunk):
-                shares[(r, chunk)] = part[:, (chunk - first_chunk) * CHUNK : (chunk - first_chunk + 1) * CHUNK]
+        def make_shares(r, first, end):
+            nc.vector.tensor_scalar(shares[r][:, first:end], exps[r][:, first:end], row_inv[:, r : r + 1], None, ALU.mult)
 
         nc.vector.reciprocal(row_inv[:, 0:2], row_sum01[:])
-        nc.vector.tensor_tensor(factor[:, 0:2], row_inv[:, 0:2], key_scale[:, 0:2], ALU.mult)
-        nc.vector.reciprocal(row_inv[:, 2:3], row_sum[2])
-        nc.vector.reciprocal(row_inv[:, 3:4], row_sum[3])
-        make_shares(3, 0, 1)
-        make_shares(2, 0, 1)
-        make_shares(0, 0, CHUNKS)
-        make_shares(1, 0, CHUNKS)
-        nc.vector.tensor_tensor(factor[:, 2:4], row_inv[:, 2:4], key_scale[:, 2:4], ALU.mult)
-        make_shares(2, 1, CHUNKS)
-        make_shares(3, 1, CHUNKS)
+        quantise_mv(0)
+        make_shares(0, 0, I)
+        make_shares(1, 0, I)
+        nc.vector.reciprocal(row_inv[:, 2:4], row_sum23[:])
+        make_shares(2, 0, CHUNK)
+        make_shares(3, 0, CHUNK)
+        make_shares(3, CHUNK, I)
+        make_shares(2, CHUNK, I)
+        quantise_mv(1)
 
         scaled = [sbuf("scaled%d" % half, [P, PACK, HALF], F32) for half in range(2)]
 
-        def scale_half(half):
-            for r in range(PACK):
-                slots = slice(half * HALF, (half + 1) * HALF)
-                nc.scalar.activation(scaled[half][:, r, :], exps[r][:, slots], ACT.Copy, scale=factor[:, r : r + 1])
+        def scale_shares(r, first, end):
+            half = first // HALF
+            target = scaled[half][:, r, first - half * HALF : end - half * HALF]
+            nc.scalar.activation(target, shares[r][:, first:end], ACT.Copy, scale=key_scale[:, r : r + 1])
 
-        scale_half(0)
+        scale_shares(0, 0, HALF)
+        scale_shares(1, 0, HALF)
+        scale_shares(2, 0, CHUNK)
+        scale_shares(3, 0, CHUNK)
+        scale_shares(3, CHUNK, HALF)
+        scale_shares(2, CHUNK, HALF)
 
         warm_up = bank("warm_up", [P, I], 1)
         for repeat in range(2):
@@ -166,54 +190,39 @@ def tile_attend_externalattn_kernel(tc, tok_words, tok_scales, mk, msc, mv, offs
         turned = []
         for chunk in range(CHUNKS):
             turned_bank = bank("turned%d" % chunk, [P, P], TURNED_BANK + chunk)
-            for r in range(PACK):
+            order = (0, 1, 2, 3) if chunk == 0 else (0, 1, 3, 2)
+            for step, r in enumerate(order):
                 nc.tensor.matmul(
-                    turned_bank[:], shares[(r, chunk)], identity[:],
-                    start=(r == 0), stop=(r == PACK - 1), is_transpose=True,
+                    turned_bank[:], shares[r][:, chunk * CHUNK : (chunk + 1) * CHUNK], identity[:],
+                    start=(step == 0), stop=(step == PACK - 1), is_transpose=True,
                 )
             turned.append(turned_bank)
         col_inv = []
         for chunk in range(2):
             col_sum = sbuf("col_sum%d" % chunk, [P, 1], F32)
             nc.vector.tensor_reduce(col_sum[:], turned[chunk][:], AX.X, ALU.add)
+            if chunk == 0:
+                quantise_mv(2)
             inverse = sbuf("col_inv%d" % chunk, [P, 1], F32)
             nc.vector.reciprocal(inverse[:], col_sum[:])
             col_inv.append(inverse[:])
+        quantise_mv(3)
         col_sum23 = sbuf("col_sum23", [P, 2], F32)
         for chunk in range(2, CHUNKS):
             by_product = sbuf("by_product%d" % chunk, [P, P], F32)
             nc.scalar.activation(by_product[:], turned[chunk][:], ACT.Copy, accum_out=col_sum23[:, chunk - 2 : chunk - 1])
-        col_inv23 = sbuf("col_inv23", [P, 2], F32)
-        nc.vector.reciprocal(col_inv23[:], col_sum23[:])
-        col_inv.extend([col_inv23[:, 0:1], col_inv23[:, 1:2]])
+        for r in range(PACK):
+            scale_shares(r, HALF, I)
+
         spread = []
-        for chunk in range(CHUNKS):
+
+        def spread_inverse(chunk):
             spread_bank = bank("spread%d" % chunk, [P, CHUNK], chunk)
             nc.tensor.transpose(spread_bank[:], col_inv[chunk].to_broadcast([P, P]), identity[:])
             spread.append(spread_bank)
-        scale_half(1)
 
-        mv_codes = []
-        mv_scales = []
-        for half in range(2):
-            mv_grouped = sbuf("mv_grouped%d" % half, [P, HALF, PACK], BF16)
-            if half == 0:
-                nc.scalar.copy(
-                    mv_grouped[:].rearrange("p (g n) t -> p g t n", n=RUN),
-                    mv_raw[half][:].rearrange("p t (g n) -> p g t n", n=RUN),
-                )
-            else:
-                nc.gpsimd.tensor_scalar(
-                    mv_grouped[:], mv_raw[half][:].rearrange("p t e -> p e t"), 1.0, 0.0, ALU.mult, ALU.add
-                )
-            codes = sbuf("mv_codes%d" % half, [P, HALF], U32, tag="last_row_max" if half == 0 else "last_row_sum")
-            scales = sbuf("mv_scales%d" % half, [P, HALF], U8)
-            nc.vector.quantize_mx(
-                out=codes[:].bitcast(FP8X4), scales=scales[:], in_=mv_grouped[:].rearrange("p e t -> p (e t)")
-            )
-            for first in range(0, HALF, P):
-                mv_codes.append(codes[:, first : first + P])
-                mv_scales.append(scales[:, first : first + P])
+        spread_inverse(0)
+        spread_inverse(1)
 
         out_rows = out.rearrange("(b p) i -> p b i", p=P)
         for chunk in range(CHUNKS):
@@ -229,6 +238,12 @@ def tile_attend_externalattn_kernel(tc, tok_words, tok_scales, mk, msc, mv, offs
                     inverse_sums.unsqueeze(2).to_broadcast([P, width // RUN, PACK, RUN]),
                     ALU.mult,
                 )
+            if chunk == 0:
+                col_inv23 = sbuf("col_inv23", [P, 2], F32, tag="col_inv0")
+                nc.vector.reciprocal(col_inv23[:], col_sum23[:])
+                col_inv.extend([col_inv23[:, 0:1], col_inv23[:, 1:2]])
+                spread_inverse(2)
+                spread_inverse(3)
             w_codes = sbuf("w_codes%d" % chunk, [P, CHUNK], U32)
             w_scales = sbuf("w_scales%d" % chunk, [P, CHUNK], U8)
             nc.vector.quantize_mx(

@@ -27,7 +27,7 @@ HALF = 256
 CHUNK = 128
 CHUNKS = I // CHUNK
 RUN = 4
-MK_PIECES = ((0, 256), (256, 384), (384, 512))
+MK_PIECES = ((0, 384), (384, 512))
 GROUPS = E // P
 TURNED_BANK = PACK
 
@@ -88,7 +88,7 @@ def tile_attend_externalattn_kernel(tc, tok_words, tok_scales, mk, msc, mv, offs
                 by_operand = mk_raw[piece][:].rearrange("p t (c r) -> p c t r", r=PACK)
                 target = mk_grouped[pair][:, :, first // PACK : end // PACK, :].rearrange("p r c t -> p c t r")
                 source = by_operand[:, :, :, 2 * pair : 2 * pair + 2]
-                if piece == 0 or (piece == 1 and pair == 0) or (piece == 2 and pair == 1):
+                if piece == 0:
                     nc.scalar.copy(target, source)
                 else:
                     nc.vector.tensor_copy(target, source)
@@ -155,11 +155,11 @@ def tile_attend_externalattn_kernel(tc, tok_words, tok_scales, mk, msc, mv, offs
         make_shares(0, 0, I)
         make_shares(1, 0, I)
         nc.vector.reciprocal(row_inv[:, 2:4], row_sum23[:])
+        quantise_mv(1)
         make_shares(2, 0, CHUNK)
         make_shares(3, 0, CHUNK)
         make_shares(3, CHUNK, I)
         make_shares(2, CHUNK, I)
-        quantise_mv(1)
 
         scaled = [sbuf("scaled%d" % half, [P, PACK, HALF], F32) for half in range(2)]
 
@@ -206,11 +206,11 @@ def tile_attend_externalattn_kernel(tc, tok_words, tok_scales, mk, msc, mv, offs
             inverse = sbuf("col_inv%d" % chunk, [P, 1], F32)
             nc.vector.reciprocal(inverse[:], col_sum[:])
             col_inv.append(inverse[:])
-        quantise_mv(3)
+            if chunk == 0:
+                quantise_mv(3)
         col_sum23 = sbuf("col_sum23", [P, 2], F32)
         for chunk in range(2, CHUNKS):
-            by_product = sbuf("by_product%d" % chunk, [P, P], F32)
-            nc.scalar.activation(by_product[:], turned[chunk][:], ACT.Copy, accum_out=col_sum23[:, chunk - 2 : chunk - 1])
+            nc.vector.tensor_reduce(col_sum23[:, chunk - 2 : chunk - 1], turned[chunk][:], AX.X, ALU.add)
         for r in range(PACK):
             scale_shares(r, HALF, I)
 
@@ -263,7 +263,7 @@ def tile_attend_externalattn_kernel(tc, tok_words, tok_scales, mk, msc, mv, offs
                         stop=True,
                     )
                 result = sbuf("result%d_%d" % (chunk, side), [P, 2, CHUNK], F32)
-                if chunk == CHUNKS - 1 and side == 1:
+                if chunk >= CHUNKS - 2 and side == 1:
                     nc.vector.tensor_copy(result[:], sums[:])
                 else:
                     nc.scalar.copy(result[:], sums[:])

@@ -175,18 +175,6 @@ def tile_attend_externalattn_kernel(tc, tok_words, tok_scales, mk, msc, mv, offs
         scale_shares(3, CHUNK, HALF)
         scale_shares(2, CHUNK, HALF)
 
-        warm_up = bank("warm_up", [P, I], 1)
-        for repeat in range(2):
-            nc.tensor.matmul_mx(
-                out=warm_up[:],
-                lhsT=mk_codes[0][:].bitcast(FP8X4),
-                lhsT_scale=mk_scales[0][:],
-                rhs=token_words[:].bitcast(FP4X4),
-                rhs_scale=token_scales[:],
-                start=(repeat == 0),
-                stop=(repeat == 1),
-            )
-
         turned = []
         for chunk in range(CHUNKS):
             turned_bank = bank("turned%d" % chunk, [P, P], TURNED_BANK + chunk)

@@ -27,8 +27,9 @@ HALF = 256
 CHUNK = 128
 CHUNKS = I // CHUNK
 RUN = 4
-MK_PIECES = ((0, 384), (384, 512))
+MK_PIECES = ((0, 320), (320, 512))
 GROUPS = E // P
+SCALAR_GROUPS = 2
 TURNED_BANK = PACK
 
 
@@ -101,8 +102,9 @@ def tile_attend_externalattn_kernel(tc, tok_words, tok_scales, mk, msc, mv, offs
 
         mv_grouped = []
         for group in range(GROUPS):
-            grouped = sbuf("mv_grouped%d" % group, [P, P, PACK], BF16)
-            if group < 2:
+            tag = "mk_grouped1" if group == SCALAR_GROUPS else None
+            grouped = sbuf("mv_grouped%d" % group, [P, P, PACK], BF16, tag=tag)
+            if group < SCALAR_GROUPS:
                 nc.scalar.copy(
                     grouped[:].rearrange("p (g n) t -> p g t n", n=RUN),
                     mv_raw[group][:].rearrange("p t (g n) -> p g t n", n=RUN),
@@ -116,8 +118,8 @@ def tile_attend_externalattn_kernel(tc, tok_words, tok_scales, mk, msc, mv, offs
         mv_codes = []
         mv_scales = []
 
-        def quantise_mv(group):
-            codes = sbuf("mv_codes%d" % group, [P, P], U32, tag=("row_max1", "row_max3", "row_sum23", "col_sum0")[group])
+        def quantise_mv(group, on_bytes_of):
+            codes = sbuf("mv_codes%d" % group, [P, P], U32, tag=on_bytes_of)
             scales = sbuf("mv_scales%d" % group, [P, P], U8)
             nc.vector.quantize_mx(
                 out=codes[:].bitcast(FP8X4), scales=scales[:], in_=mv_grouped[group][:].rearrange("p e t -> p (e t)")
@@ -140,7 +142,7 @@ def tile_attend_externalattn_kernel(tc, tok_words, tok_scales, mk, msc, mv, offs
                 start=True,
                 stop=True,
             )
-            neg_max = sbuf("neg_max%d" % r, [P, 1], F32, tag="row_max%d" % r)
+            neg_max = sbuf("neg_max%d" % r, [P, 1], F32)
             nc.vector.tensor_reduce(neg_max[:], scores[:], AX.X, ALU.max, negate=True)
             nc.scalar.activation(exps[r][:], scores[:], ACT.Exp, bias=neg_max[:], scale=1.0, accum_out=row_sum[r])
 
@@ -151,11 +153,11 @@ def tile_attend_externalattn_kernel(tc, tok_words, tok_scales, mk, msc, mv, offs
             nc.vector.tensor_scalar(shares[r][:, first:end], exps[r][:, first:end], row_inv[:, r : r + 1], None, ALU.mult)
 
         nc.vector.reciprocal(row_inv[:, 0:2], row_sum01[:])
-        quantise_mv(0)
+        quantise_mv(0, "neg_max1")
         make_shares(0, 0, I)
         make_shares(1, 0, I)
         nc.vector.reciprocal(row_inv[:, 2:4], row_sum23[:])
-        quantise_mv(1)
+        quantise_mv(1, "neg_max3")
         make_shares(2, 0, CHUNK)
         make_shares(3, 0, CHUNK)
         make_shares(3, CHUNK, I)
@@ -185,17 +187,16 @@ def tile_attend_externalattn_kernel(tc, tok_words, tok_scales, mk, msc, mv, offs
                     start=(step == 0), stop=(step == PACK - 1), is_transpose=True,
                 )
             turned.append(turned_bank)
-        col_inv = []
-        for chunk in range(2):
-            col_sum = sbuf("col_sum%d" % chunk, [P, 1], F32)
-            nc.vector.tensor_reduce(col_sum[:], turned[chunk][:], AX.X, ALU.add)
-            if chunk == 0:
-                quantise_mv(2)
-            inverse = sbuf("col_inv%d" % chunk, [P, 1], F32)
-            nc.vector.reciprocal(inverse[:], col_sum[:])
-            col_inv.append(inverse[:])
-            if chunk == 0:
-                quantise_mv(3)
+        col_sum0 = sbuf("col_sum0", [P, 1], F32)
+        nc.vector.tensor_reduce(col_sum0[:], turned[0][:], AX.X, ALU.add)
+        quantise_mv(2, "row_sum23")
+        col_inv0 = sbuf("col_inv0", [P, 1], F32)
+        nc.vector.reciprocal(col_inv0[:], col_sum0[:])
+        quantise_mv(3, "col_sum0")
+        col_sum1 = sbuf("col_sum1", [P, 1], F32)
+        nc.vector.tensor_reduce(col_sum1[:], turned[1][:], AX.X, ALU.add)
+        col_inv1 = sbuf("col_inv1", [P, 1], F32)
+        nc.vector.reciprocal(col_inv1[:], col_sum1[:])
         col_sum23 = sbuf("col_sum23", [P, 2], F32)
         for chunk in range(2, CHUNKS):
             nc.vector.tensor_reduce(col_sum23[:, chunk - 2 : chunk - 1], turned[chunk][:], AX.X, ALU.add)
@@ -204,13 +205,13 @@ def tile_attend_externalattn_kernel(tc, tok_words, tok_scales, mk, msc, mv, offs
 
         spread = []
 
-        def spread_inverse(chunk):
+        def spread_inverse(chunk, inverse):
             spread_bank = bank("spread%d" % chunk, [P, CHUNK], chunk)
-            nc.tensor.transpose(spread_bank[:], col_inv[chunk].to_broadcast([P, P]), identity[:])
+            nc.tensor.transpose(spread_bank[:], inverse.to_broadcast([P, P]), identity[:])
             spread.append(spread_bank)
 
-        spread_inverse(0)
-        spread_inverse(1)
+        spread_inverse(0, col_inv0[:])
+        spread_inverse(1, col_inv1[:])
 
         out_rows = out.rearrange("(b p) i -> p b i", p=P)
         for chunk in range(CHUNKS):
@@ -229,9 +230,8 @@ def tile_attend_externalattn_kernel(tc, tok_words, tok_scales, mk, msc, mv, offs
             if chunk == 0:
                 col_inv23 = sbuf("col_inv23", [P, 2], F32, tag="col_inv0")
                 nc.vector.reciprocal(col_inv23[:], col_sum23[:])
-                col_inv.extend([col_inv23[:, 0:1], col_inv23[:, 1:2]])
-                spread_inverse(2)
-                spread_inverse(3)
+                spread_inverse(2, col_inv23[:, 0:1])
+                spread_inverse(3, col_inv23[:, 1:2])
             w_codes = sbuf("w_codes%d" % chunk, [P, CHUNK], U32)
             w_scales = sbuf("w_scales%d" % chunk, [P, CHUNK], U8)
             nc.vector.quantize_mx(

@@ -30,6 +30,7 @@ RUN = 4
 MK_PIECES = ((0, 320), (320, 512))
 GROUPS = E // P
 SCALAR_GROUPS = 2
+WARM_UP_PASSES = 2
 TURNED_BANK = PACK
 
 
@@ -145,6 +146,18 @@ def tile_attend_externalattn_kernel(tc, tok_words, tok_scales, mk, msc, mv, offs
             neg_max = sbuf("neg_max%d" % r, [P, 1], F32)
             nc.vector.tensor_reduce(neg_max[:], scores[:], AX.X, ALU.max, negate=True)
             nc.scalar.activation(exps[r][:], scores[:], ACT.Exp, bias=neg_max[:], scale=1.0, accum_out=row_sum[r])
+
+        for repeat in range(WARM_UP_PASSES):
+            unread = bank("unread%d" % repeat, [P, I], 1)
+            nc.tensor.matmul_mx(
+                out=unread[:],
+                lhsT=mk_codes[repeat][:].bitcast(FP8X4),
+                lhsT_scale=mk_scales[repeat][:],
+                rhs=token_words[:].bitcast(FP4X4),
+                rhs_scale=token_scales[:],
+                start=True,
+                stop=True,
+            )
 
         row_inv = sbuf("row_inv", [P, PACK], F32)
         shares = [sbuf("shares%d" % r, [P, I], F32) for r in range(PACK)]

@@ -162,17 +162,24 @@ def tile_attend_externalattn_kernel(tc, tok_words, tok_scales, mk, msc, mv, offs
         row_inv = sbuf("row_inv", [P, PACK], F32)
         shares = [sbuf("shares%d" % r, [P, I], F32) for r in range(PACK)]
 
+        def share_piece(r, first, end):
+            if r == 1 and first >= CHUNK:
+                return rest1[:, first - CHUNK : end - CHUNK]
+            return shares[r][:, first:end]
+
         def make_shares(r, first, end):
             nc.vector.tensor_scalar(shares[r][:, first:end], exps[r][:, first:end], row_inv[:, r : r + 1], None, ALU.mult)
 
         nc.vector.reciprocal(row_inv[:, 0:2], row_sum01[:])
         quantise_mv(0, "neg_max1")
         make_shares(0, 0, I)
-        make_shares(1, 0, I)
+        make_shares(1, 0, CHUNK)
         nc.vector.reciprocal(row_inv[:, 2:4], row_sum23[:])
         quantise_mv(1, "neg_max3")
         make_shares(2, 0, CHUNK)
         make_shares(3, 0, CHUNK)
+        rest1 = sbuf("rest1", [P, I - CHUNK], F32, tag="row_sum23")
+        nc.vector.tensor_scalar(rest1[:], exps[1][:, CHUNK:I], row_inv[:, 1:2], None, ALU.mult)
         make_shares(3, CHUNK, I)
         make_shares(2, CHUNK, I)
 
@@ -181,12 +188,13 @@ def tile_attend_externalattn_kernel(tc, tok_words, tok_scales, mk, msc, mv, offs
         def scale_shares(r, first, end):
             half = first // HALF
             target = scaled[half][:, r, first - half * HALF : end - half * HALF]
-            nc.scalar.activation(target, shares[r][:, first:end], ACT.Copy, scale=key_scale[:, r : r + 1])
+            nc.scalar.activation(target, share_piece(r, first, end), ACT.Copy, scale=key_scale[:, r : r + 1])
 
         scale_shares(0, 0, HALF)
-        scale_shares(1, 0, HALF)
+        scale_shares(1, 0, CHUNK)
         scale_shares(2, 0, CHUNK)
         scale_shares(3, 0, CHUNK)
+        scale_shares(1, CHUNK, HALF)
         scale_shares(3, CHUNK, HALF)
         scale_shares(2, CHUNK, HALF)
 
@@ -196,13 +204,13 @@ def tile_attend_externalattn_kernel(tc, tok_words, tok_scales, mk, msc, mv, offs
             order = (0, 1, 2, 3) if chunk == 0 else (0, 1, 3, 2)
             for step, r in enumerate(order):
                 nc.tensor.matmul(
-                    turned_bank[:], shares[r][:, chunk * CHUNK : (chunk + 1) * CHUNK], identity[:],
+                    turned_bank[:], share_piece(r, chunk * CHUNK, (chunk + 1) * CHUNK), identity[:],
                     start=(step == 0), stop=(step == PACK - 1), is_transpose=True,
                 )
             turned.append(turned_bank)
         col_sum0 = sbuf("col_sum0", [P, 1], F32)
         nc.vector.tensor_reduce(col_sum0[:], turned[0][:], AX.X, ALU.add)
-        quantise_mv(2, "row_sum23")
+        quantise_mv(2, "exps1")
         col_inv0 = sbuf("col_inv0", [P, 1], F32)
         nc.vector.reciprocal(col_inv0[:], col_sum0[:])
         quantise_mv(3, "col_sum0")
@@ -211,9 +219,12 @@ def tile_attend_externalattn_kernel(tc, tok_words, tok_scales, mk, msc, mv, offs
         col_inv1 = sbuf("col_inv1", [P, 1], F32)
         nc.vector.reciprocal(col_inv1[:], col_sum1[:])
         col_sum23 = sbuf("col_sum23", [P, 2], F32)
+        for r in range(2):
+            scale_shares(r, HALF, I)
         for chunk in range(2, CHUNKS):
-            nc.vector.tensor_reduce(col_sum23[:, chunk - 2 : chunk - 1], turned[chunk][:], AX.X, ALU.add)
-        for r in range(PACK):
+            copied = sbuf("copied%d" % chunk, [P, P], BF16)
+            nc.scalar.activation(copied[:], turned[chunk][:], ACT.Copy, accum_out=col_sum23[:, chunk - 2 : chunk - 1])
+        for r in range(2, PACK):
             scale_shares(r, HALF, I)
 
         spread = []
@@ -247,9 +258,13 @@ def tile_attend_externalattn_kernel(tc, tok_words, tok_scales, mk, msc, mv, offs
                 spread_inverse(3, col_inv23[:, 1:2])
             w_codes = sbuf("w_codes%d" % chunk, [P, CHUNK], U32)
             w_scales = sbuf("w_scales%d" % chunk, [P, CHUNK], U8)
-            nc.vector.quantize_mx(
-                out=w_codes[:].bitcast(FP8X4), scales=w_scales[:], in_=weights[:].rearrange("p i r -> p (i r)")
-            )
+            step = CHUNK // 2 if chunk == CHUNKS - 1 else CHUNK
+            for first in range(0, CHUNK, step):
+                nc.vector.quantize_mx(
+                    out=w_codes[:, first : first + step].bitcast(FP8X4),
+                    scales=w_scales[:, first : first + step],
+                    in_=weights[:, first : first + step].rearrange("p i r -> p (i r)"),
+                )
             for side in range(2):
                 sums = bank("sums%d_%d" % (chunk, side), [P, 2, CHUNK], TURNED_BANK + chunk if side == 0 else chunk)
                 for in_bank in range(2):

@@ -219,12 +219,9 @@ def tile_attend_externalattn_kernel(tc, tok_words, tok_scales, mk, msc, mv, offs
         col_inv1 = sbuf("col_inv1", [P, 1], F32)
         nc.vector.reciprocal(col_inv1[:], col_sum1[:])
         col_sum23 = sbuf("col_sum23", [P, 2], F32)
-        for r in range(2):
-            scale_shares(r, HALF, I)
         for chunk in range(2, CHUNKS):
-            copied = sbuf("copied%d" % chunk, [P, P], BF16)
-            nc.scalar.activation(copied[:], turned[chunk][:], ACT.Copy, accum_out=col_sum23[:, chunk - 2 : chunk - 1])
-        for r in range(2, PACK):
+            nc.vector.tensor_reduce(col_sum23[:, chunk - 2 : chunk - 1], turned[chunk][:], AX.X, ALU.add)
+        for r in range(PACK):
             scale_shares(r, HALF, I)
 
         spread = []

@@ -101,20 +101,22 @@ def tile_attend_externalattn_kernel(tc, tok_words, tok_scales, mk, msc, mv, offs
                     in_=mk_grouped[pair][:, in_pair].rearrange("p c t -> p (c t)"),
                 )
 
-        mv_grouped = []
-        for group in range(GROUPS):
-            tag = "mk_grouped1" if group == SCALAR_GROUPS else None
-            grouped = sbuf("mv_grouped%d" % group, [P, P, PACK], BF16, tag=tag)
-            if group < SCALAR_GROUPS:
-                nc.scalar.copy(
-                    grouped[:].rearrange("p (g n) t -> p g t n", n=RUN),
-                    mv_raw[group][:].rearrange("p t (g n) -> p g t n", n=RUN),
-                )
-            else:
-                nc.gpsimd.tensor_scalar(
-                    grouped[:], mv_raw[group][:].rearrange("p t e -> p e t"), 1.0, 0.0, ALU.mult, ALU.add
-                )
-            mv_grouped.append(grouped)
+        mv_grouped = {}
+
+        def interleave_mv(group, copy):
+            grouped = sbuf("mv_grouped%d" % group, [P, P, PACK], BF16)
+            copy(
+                grouped[:].rearrange("p (g n) t -> p g t n", n=RUN),
+                mv_raw[group][:].rearrange("p t (g n) -> p g t n", n=RUN),
+            )
+            mv_grouped[group] = grouped
+
+        for group in range(SCALAR_GROUPS):
+            interleave_mv(group, nc.scalar.copy)
+        mv_grouped[SCALAR_GROUPS] = sbuf("mv_grouped%d" % SCALAR_GROUPS, [P, P, PACK], BF16, tag="mk_grouped1")
+        nc.gpsimd.tensor_scalar(
+            mv_grouped[SCALAR_GROUPS][:], mv_raw[SCALAR_GROUPS][:].rearrange("p t e -> p e t"), 1.0, 0.0, ALU.mult, ALU.add
+        )
 
         mv_codes = []
         mv_scales = []
@@ -174,6 +176,7 @@ def tile_attend_externalattn_kernel(tc, tok_words, tok_scales, mk, msc, mv, offs
         quantise_mv(0, "neg_max1")
         make_shares(0, 0, I)
         make_shares(1, 0, CHUNK)
+        interleave_mv(GROUPS - 1, nc.vector.tensor_copy)
         nc.vector.reciprocal(row_inv[:, 2:4], row_sum23[:])
         quantise_mv(1, "neg_max3")
         make_shares(2, 0, CHUNK)

@@ -39,6 +39,7 @@ def tile_attend_externalattn_kernel(tc, tok_words, tok_scales, mk, msc, mv, offs
     with ExitStack() as ctx:
         keep = ctx.enter_context(tc.tile_pool(name="keep", bufs=1))
         psum = ctx.enter_context(tc.psum_pool(name="psum", bufs=1))
+        placed = ctx.enter_context(tc.tile_pool(name="placed", bufs=1))
 
         def sbuf(name, shape, dtype, tag=None):
             return keep.tile(shape, dtype, name=name, tag=tag or name, align_bytes=64)
@@ -122,7 +123,10 @@ def tile_attend_externalattn_kernel(tc, tok_words, tok_scales, mk, msc, mv, offs
         mv_scales = []
 
         def quantise_mv(group, on_bytes_of):
-            codes = sbuf("mv_codes%d" % group, [P, P], U32, tag=on_bytes_of)
+            if on_bytes_of is None:
+                codes = placed.tile([P, P], U32, name="mv_codes%d" % group, offset=0, align_bytes=64)
+            else:
+                codes = sbuf("mv_codes%d" % group, [P, P], U32, tag=on_bytes_of)
             scales = sbuf("mv_scales%d" % group, [P, P], U8)
             nc.vector.quantize_mx(
                 out=codes[:].bitcast(FP8X4), scales=scales[:], in_=mv_grouped[group][:].rearrange("p e t -> p (e t)")
@@ -132,8 +136,9 @@ def tile_attend_externalattn_kernel(tc, tok_words, tok_scales, mk, msc, mv, offs
 
         exps = [sbuf("exps%d" % r, [P, I], F32) for r in range(PACK)]
         row_sum01 = sbuf("row_sum01", [P, 2], F32)
-        row_sum23 = sbuf("row_sum23", [P, 2], F32)
-        row_sum = [row_sum01[:, 0:1], row_sum01[:, 1:2], row_sum23[:, 0:1], row_sum23[:, 1:2]]
+        row_sum2 = sbuf("row_sum2", [P, 1], F32)
+        row_sum3 = sbuf("row_sum3", [P, 1], F32)
+        row_sum = [row_sum01[:, 0:1], row_sum01[:, 1:2], row_sum2[:], row_sum3[:]]
         for r in range(PACK):
             scores = bank("scores%d" % r, [P, I], r)
             nc.tensor.matmul_mx(
@@ -166,25 +171,30 @@ def tile_attend_externalattn_kernel(tc, tok_words, tok_scales, mk, msc, mv, offs
 
         def share_piece(r, first, end):
             if r == 1 and first >= CHUNK:
-                return rest1[:, first - CHUNK : end - CHUNK]
+                return late[:, first - CHUNK : end - CHUNK]
             return shares[r][:, first:end]
 
         def make_shares(r, first, end):
-            nc.vector.tensor_scalar(shares[r][:, first:end], exps[r][:, first:end], row_inv[:, r : r + 1], None, ALU.mult)
+            nc.vector.tensor_scalar(share_piece(r, first, end), exps[r][:, first:end], row_inv[:, r : r + 1], None, ALU.mult)
 
         nc.vector.reciprocal(row_inv[:, 0:2], row_sum01[:])
         quantise_mv(0, "neg_max1")
         make_shares(0, 0, I)
+        nc.vector.reciprocal(row_inv[:, 2:3], row_sum2[:])
         make_shares(1, 0, CHUNK)
-        interleave_mv(GROUPS - 1, nc.vector.tensor_copy)
-        nc.vector.reciprocal(row_inv[:, 2:4], row_sum23[:])
-        quantise_mv(1, "neg_max3")
+        quantise_mv(1, "row_sum01")
         make_shares(2, 0, CHUNK)
+        nc.scalar.activation(shares[2][:, CHUNK:I], exps[2][:, CHUNK:I], ACT.Copy, scale=row_inv[:, 2:3])
+        nc.vector.reciprocal(row_inv[:, 3:4], row_sum3[:])
+        quantise_mv(2, "neg_max3")
         make_shares(3, 0, CHUNK)
-        rest1 = sbuf("rest1", [P, I - CHUNK], F32, tag="row_sum23")
-        nc.vector.tensor_scalar(rest1[:], exps[1][:, CHUNK:I], row_inv[:, 1:2], None, ALU.mult)
+        late = sbuf("late", [P, I - CHUNK], F32, tag="row_sum3")
+        make_shares(1, CHUNK, I)
         make_shares(3, CHUNK, I)
-        make_shares(2, CHUNK, I)
+        mv_grouped[GROUPS - 1] = sbuf("mv_grouped%d" % (GROUPS - 1), [P, P, PACK], BF16, tag="exps3")
+        nc.gpsimd.tensor_scalar(
+            mv_grouped[GROUPS - 1][:], mv_raw[GROUPS - 1][:].rearrange("p t e -> p e t"), 1.0, 0.0, ALU.mult, ALU.add
+        )
 
         scaled = [sbuf("scaled%d" % half, [P, PACK, HALF], F32) for half in range(2)]
 
@@ -195,11 +205,10 @@ def tile_attend_externalattn_kernel(tc, tok_words, tok_scales, mk, msc, mv, offs
 
         scale_shares(0, 0, HALF)
         scale_shares(1, 0, CHUNK)
-        scale_shares(2, 0, CHUNK)
+        scale_shares(2, 0, HALF)
         scale_shares(3, 0, CHUNK)
         scale_shares(1, CHUNK, HALF)
         scale_shares(3, CHUNK, HALF)
-        scale_shares(2, CHUNK, HALF)
 
         turned = []
         for chunk in range(CHUNKS):
@@ -213,10 +222,8 @@ def tile_attend_externalattn_kernel(tc, tok_words, tok_scales, mk, msc, mv, offs
             turned.append(turned_bank)
         col_sum0 = sbuf("col_sum0", [P, 1], F32)
         nc.vector.tensor_reduce(col_sum0[:], turned[0][:], AX.X, ALU.add)
-        quantise_mv(2, "exps1")
-        col_inv0 = sbuf("col_inv0", [P, 1], F32)
-        nc.vector.reciprocal(col_inv0[:], col_sum0[:])
-        quantise_mv(3, "col_sum0")
+        col_inv0 = placed.tile([P, P + 16], F32, name="col_inv0", offset=0, align_bytes=64)
+        nc.vector.reciprocal(col_inv0[:, 0:1], col_sum0[:])
         col_sum1 = sbuf("col_sum1", [P, 1], F32)
         nc.vector.tensor_reduce(col_sum1[:], turned[1][:], AX.X, ALU.add)
         col_inv1 = sbuf("col_inv1", [P, 1], F32)
@@ -234,7 +241,7 @@ def tile_attend_externalattn_kernel(tc, tok_words, tok_scales, mk, msc, mv, offs
             nc.tensor.transpose(spread_bank[:], inverse.to_broadcast([P, P]), identity[:])
             spread.append(spread_bank)
 
-        spread_inverse(0, col_inv0[:])
+        spread_inverse(0, col_inv0[:, 0:1])
         spread_inverse(1, col_inv1[:])
 
         out_rows = out.rearrange("(b p) i -> p b i", p=P)
@@ -252,8 +259,9 @@ def tile_attend_externalattn_kernel(tc, tok_words, tok_scales, mk, msc, mv, offs
                     ALU.mult,
                 )
             if chunk == 0:
-                col_inv23 = sbuf("col_inv23", [P, 2], F32, tag="col_inv0")
+                col_inv23 = placed.tile([P, 2], F32, name="col_inv23", offset=4 * P, align_bytes=64)
                 nc.vector.reciprocal(col_inv23[:], col_sum23[:])
+                quantise_mv(3, None)
                 spread_inverse(2, col_inv23[:, 0:1])
                 spread_inverse(3, col_inv23[:, 1:2])
             w_codes = sbuf("w_codes%d" % chunk, [P, CHUNK], U32)

@@ -28,6 +28,7 @@ CHUNK = 128
 CHUNKS = I // CHUNK
 RUN = 4
 MK_PIECES = ((0, 320), (320, 512))
+DMA_ALIGN = 256
 GROUPS = E // P
 SCALAR_GROUPS = 2
 WARM_UP_PASSES = 2
@@ -42,7 +43,7 @@ def tile_attend_externalattn_kernel(tc, tok_words, tok_scales, mk, msc, mv, offs
         placed = ctx.enter_context(tc.tile_pool(name="placed", bufs=1))
 
         def sbuf(name, shape, dtype, tag=None):
-            return keep.tile(shape, dtype, name=name, tag=tag or name, align_bytes=64)
+            return keep.tile(shape, dtype, name=name, tag=tag or name, align_bytes=DMA_ALIGN)
 
         def bank(name, shape, number):
             return psum.tile(shape, F32, name=name, tag="bank%d" % number)

@@ -29,6 +29,9 @@ CHUNKS = I // CHUNK
 RUN = 4
 MK_PIECES = ((0, 320), (320, 512))
 DMA_ALIGN = 256
+CUT = MK_PIECES[0][1] // PACK
+WHILE_WAITING = 24
+SCALAR_LATE = 16
 GROUPS = E // P
 SCALAR_GROUPS = 2
 WARM_UP_PASSES = 2
@@ -87,21 +90,32 @@ def tile_attend_externalattn_kernel(tc, tok_words, tok_scales, mk, msc, mv, offs
         mk_codes = [sbuf("mk_codes%d" % r, [P, P], U32) for r in range(PACK)]
         mk_scales = [sbuf("mk_scales%d" % r, [P, P], U8) for r in range(PACK)]
         mk_grouped = [sbuf("mk_grouped%d" % pair, [P, 2, P, PACK], BF16) for pair in range(2)]
-        for pair in range(2):
-            for piece, (first, end) in enumerate(MK_PIECES):
-                by_operand = mk_raw[piece][:].rearrange("p t (c r) -> p c t r", r=PACK)
-                target = mk_grouped[pair][:, :, first // PACK : end // PACK, :].rearrange("p r c t -> p c t r")
-                source = by_operand[:, :, :, 2 * pair : 2 * pair + 2]
-                if piece == 0:
-                    nc.scalar.copy(target, source)
-                else:
-                    nc.vector.tensor_copy(target, source)
-            for in_pair in range(2):
-                nc.vector.quantize_mx(
-                    out=mk_codes[2 * pair + in_pair][:].bitcast(FP8X4),
-                    scales=mk_scales[2 * pair + in_pair][:],
-                    in_=mk_grouped[pair][:, in_pair].rearrange("p c t -> p (c t)"),
-                )
+
+        def deal_mk(copy, pair, first, end):
+            piece = 0 if end <= CUT else 1
+            start = piece * CUT
+            by_operand = mk_raw[piece][:].rearrange("p t (c r) -> p c t r", r=PACK)
+            target = mk_grouped[pair][:, :, first:end, :].rearrange("p r c t -> p c t r")
+            copy(target, by_operand[:, first - start : end - start, :, 2 * pair : 2 * pair + 2])
+
+        def quantise_mk(r, first=0, end=P):
+            nc.vector.quantize_mx(
+                out=mk_codes[r][:, first:end].bitcast(FP8X4),
+                scales=mk_scales[r][:, first:end],
+                in_=mk_grouped[r // 2][:, r % 2, first:end].rearrange("p c t -> p (c t)"),
+            )
+
+        deal_mk(nc.scalar.copy, 0, 0, CUT)
+        deal_mk(nc.scalar.copy, 1, 0, WHILE_WAITING)
+        deal_mk(nc.vector.tensor_copy, 0, CUT, P - SCALAR_LATE)
+        quantise_mk(0, 0, P // 2)
+        deal_mk(nc.scalar.copy, 0, P - SCALAR_LATE, P)
+        deal_mk(nc.scalar.copy, 1, WHILE_WAITING, CUT)
+        quantise_mk(0, P // 2, P)
+        deal_mk(nc.vector.tensor_copy, 1, CUT, P)
+        quantise_mk(1)
+        quantise_mk(2)
+        quantise_mk(3)
 
         mv_grouped = {}
 
@@ -125,7 +139,7 @@ def tile_attend_externalattn_kernel(tc, tok_words, tok_scales, mk, msc, mv, offs
 
         def quantise_mv(group, on_bytes_of):
             if on_bytes_of is None:
-                codes = placed.tile([P, P], U32, name="mv_codes%d" % group, offset=0, align_bytes=64)
+                codes = placed.tile([P, P], U32, name="mv_codes%d" % group, offset=0, align_bytes=DMA_ALIGN)
             else:
                 codes = sbuf("mv_codes%d" % group, [P, P], U32, tag=on_bytes_of)
             scales = sbuf("mv_scales%d" % group, [P, P], U8)
@@ -223,7 +237,7 @@ def tile_attend_externalattn_kernel(tc, tok_words, tok_scales, mk, msc, mv, offs
             turned.append(turned_bank)
         col_sum0 = sbuf("col_sum0", [P, 1], F32)
         nc.vector.tensor_reduce(col_sum0[:], turned[0][:], AX.X, ALU.add)
-        col_inv0 = placed.tile([P, P + 16], F32, name="col_inv0", offset=0, align_bytes=64)
+        col_inv0 = placed.tile([P, P + 16], F32, name="col_inv0", offset=0, align_bytes=DMA_ALIGN)
         nc.vector.reciprocal(col_inv0[:, 0:1], col_sum0[:])
         col_sum1 = sbuf("col_sum1", [P, 1], F32)
         nc.vector.tensor_reduce(col_sum1[:], turned[1][:], AX.X, ALU.add)
@@ -260,7 +274,7 @@ def tile_attend_externalattn_kernel(tc, tok_words, tok_scales, mk, msc, mv, offs
                     ALU.mult,
                 )
             if chunk == 0:
-                col_inv23 = placed.tile([P, 2], F32, name="col_inv23", offset=4 * P, align_bytes=64)
+                col_inv23 = placed.tile([P, 2], F32, name="col_inv23", offset=4 * P, align_bytes=DMA_ALIGN)
                 nc.vector.reciprocal(col_inv23[:], col_sum23[:])
                 quantise_mv(3, None)
                 spread_inverse(2, col_inv23[:, 0:1])
@@ -274,22 +288,29 @@ def tile_attend_externalattn_kernel(tc, tok_words, tok_scales, mk, msc, mv, offs
                     scales=w_scales[:, first : first + step],
                     in_=weights[:, first : first + step].rearrange("p i r -> p (i r)"),
                 )
+
+            def product(target, group):
+                nc.tensor.matmul_mx(
+                    out=target,
+                    lhsT=mv_codes[group].bitcast(FP8X4),
+                    lhsT_scale=mv_scales[group],
+                    rhs=w_codes[:].bitcast(FP8X4),
+                    rhs_scale=w_scales[:],
+                    start=True,
+                    stop=True,
+                )
+
             for side in range(2):
-                sums = bank("sums%d_%d" % (chunk, side), [P, 2, CHUNK], TURNED_BANK + chunk if side == 0 else chunk)
-                for in_bank in range(2):
-                    group = 2 * side + in_bank
-                    nc.tensor.matmul_mx(
-                        out=sums[:, in_bank, :],
-                        lhsT=mv_codes[group].bitcast(FP8X4),
-                        lhsT_scale=mv_scales[group],
-                        rhs=w_codes[:].bitcast(FP8X4),
-                        rhs_scale=w_scales[:],
-                        start=True,
-                        stop=True,
-                    )
                 result = sbuf("result%d_%d" % (chunk, side), [P, 2, CHUNK], F32)
-                if chunk >= CHUNKS - 2 and side == 1:
-                    nc.vector.tensor_copy(result[:], sums[:])
-                else:
+                if chunk < CHUNKS - 1:
+                    sums = bank("sums%d_%d" % (chunk, side), [P, 2, CHUNK], TURNED_BANK + chunk if side == 0 else chunk)
+                    for in_bank in range(2):
+                        product(sums[:, in_bank, :], 2 * side + in_bank)
                     nc.scalar.copy(result[:], sums[:])
+                else:
+                    for in_pair, copy in enumerate((nc.vector.tensor_copy, nc.scalar.copy)):
+                        number = (TURNED_BANK + chunk, chunk, TURNED_BANK, 0)[2 * side + in_pair]
+                        sums = bank("sums%d_%d_%d" % (chunk, side, in_pair), [P, CHUNK], number)
+                        product(sums[:], 2 * side + in_pair)
+                        copy(result[:, in_pair, :], sums[:])
                 nc.sync.dma_start(out_rows[:, 2 * side : 2 * side + 2, slots], result[:])

@@ -206,7 +206,7 @@ def tile_attend_externalattn_kernel(tc, tok_words, tok_scales, mk, msc, mv, offs
         late = sbuf("late", [P, I - CHUNK], F32, tag="row_sum3")
         make_shares(1, CHUNK, I)
         make_shares(3, CHUNK, I)
-        mv_grouped[GROUPS - 1] = sbuf("mv_grouped%d" % (GROUPS - 1), [P, P, PACK], BF16, tag="exps3")
+        mv_grouped[GROUPS - 1] = sbuf("mv_grouped%d" % (GROUPS - 1), [P, P, PACK], BF16, tag="mk_grouped0")
         nc.gpsimd.tensor_scalar(
             mv_grouped[GROUPS - 1][:], mv_raw[GROUPS - 1][:].rearrange("p t e -> p e t"), 1.0, 0.0, ALU.mult, ALU.add
         )
@@ -243,6 +243,7 @@ def tile_attend_externalattn_kernel(tc, tok_words, tok_scales, mk, msc, mv, offs
         nc.vector.tensor_reduce(col_sum1[:], turned[1][:], AX.X, ALU.add)
         col_inv1 = sbuf("col_inv1", [P, 1], F32)
         nc.vector.reciprocal(col_inv1[:], col_sum1[:])
+        quantise_mv(3, "exps3")
         col_sum23 = sbuf("col_sum23", [P, 2], F32)
         for chunk in range(2, CHUNKS):
             nc.vector.tensor_reduce(col_sum23[:, chunk - 2 : chunk - 1], turned[chunk][:], AX.X, ALU.add)
@@ -276,7 +277,6 @@ def tile_attend_externalattn_kernel(tc, tok_words, tok_scales, mk, msc, mv, offs
             if chunk == 0:
                 col_inv23 = placed.tile([P, 2], F32, name="col_inv23", offset=4 * P, align_bytes=DMA_ALIGN)
                 nc.vector.reciprocal(col_inv23[:], col_sum23[:])
-                quantise_mv(3, None)
                 spread_inverse(2, col_inv23[:, 0:1])
                 spread_inverse(3, col_inv23[:, 1:2])
             w_codes = sbuf("w_codes%d" % chunk, [P, CHUNK], U32)

@@ -72,7 +72,9 @@ def tile_attend_externalattn_kernel(tc, tok_words, tok_scales, mk, msc, mv, offs
         mv_raw = []
         for group in range(GROUPS):
             raw = sbuf("mv_raw%d" % group, [P, PACK, P], F32)
-            nc.sync.dma_start(raw[:], mv_rows[:, :, group * P : (group + 1) * P])
+            step = PACK if group == 0 else 2
+            for first in range(0, PACK, step):
+                nc.sync.dma_start(raw[:, first : first + step], mv_rows[:, first : first + step, group * P : (group + 1) * P])
             mv_raw.append(raw)
         key_scale = sbuf("key_scale", [P, PACK], F32)
         nc.sync.dma_start(key_scale[:], msc.rearrange("(p r) o -> p (r o)", r=PACK))
@@ -211,12 +213,13 @@ def tile_attend_externalattn_kernel(tc, tok_words, tok_scales, mk, msc, mv, offs
             mv_grouped[GROUPS - 1][:], mv_raw[GROUPS - 1][:].rearrange("p t e -> p e t"), 1.0, 0.0, ALU.mult, ALU.add
         )
 
-        scaled = [sbuf("scaled%d" % half, [P, PACK, HALF], F32) for half in range(2)]
+        scaled = [sbuf("scaled%d" % half, [P, HALF // RUN, PACK, RUN], F32) for half in range(2)]
 
         def scale_shares(r, first, end):
             half = first // HALF
-            target = scaled[half][:, r, first - half * HALF : end - half * HALF]
-            nc.scalar.activation(target, share_piece(r, first, end), ACT.Copy, scale=key_scale[:, r : r + 1])
+            target = scaled[half][:, (first - half * HALF) // RUN : (end - half * HALF) // RUN, r, :]
+            source = share_piece(r, first, end).rearrange("p (g n) -> p g n", n=RUN)
+            nc.scalar.activation(target, source, ACT.Copy, scale=key_scale[:, r : r + 1])
 
         scale_shares(0, 0, HALF)
         scale_shares(1, 0, CHUNK)
@@ -270,7 +273,7 @@ def tile_attend_externalattn_kernel(tc, tok_words, tok_scales, mk, msc, mv, offs
                 inverse_sums = spread[chunk][:, first : first + width].rearrange("p (g n) -> p g n", n=RUN)
                 nc.vector.tensor_tensor(
                     weights[:, first : first + width].rearrange("p (g n) r -> p g r n", n=RUN),
-                    scaled[chunk // 2][:, :, in_half : in_half + width].rearrange("p r (g n) -> p g r n", n=RUN),
+                    scaled[chunk // 2][:, in_half // RUN : (in_half + width) // RUN],
                     inverse_sums.unsqueeze(2).to_broadcast([P, width // RUN, PACK, RUN]),
                     ALU.mult,
                 )

from contextlib import ExitStack

import concourse.mybir as mybir
from concourse.masks import make_identity

D, T, I, M, E = 512, 2048, 512, 512, 512
FLOPS = 2 * D * M * I + 2 * M * E * I

F32 = mybir.dt.float32
BF16 = mybir.dt.bfloat16
I32 = mybir.dt.int32
U32 = mybir.dt.uint32
U16 = mybir.dt.uint16
U8 = mybir.dt.uint8
FP8X4 = mybir.dt.float8_e4m3fn_x4
FP4X4 = mybir.dt.float4_e2m1fn_x4
ALU = mybir.AluOpType
ACT = mybir.ActivationFunctionType
AX = mybir.AxisListType

P = 128
PACK = 4
LIST_GROUP = 16
QUADRANT = 32
SCALE_ROWS = D // 32
HALF = 256
CHUNK = 128
CHUNKS = I // CHUNK
RUN = 4
MK_PIECES = ((0, 320), (320, 512))
DMA_ALIGN = 256
CUT = MK_PIECES[0][1] // PACK
WHILE_WAITING = 24
SCALAR_LATE = 16
GROUPS = E // P
SCALAR_GROUPS = 2
WARM_UP_PASSES = 2
TURNED_BANK = PACK


def tile_attend_externalattn_kernel(tc, tok_words, tok_scales, mk, msc, mv, offs, out):
    nc = tc.nc
    with ExitStack() as ctx:
        keep = ctx.enter_context(tc.tile_pool(name="keep", bufs=1))
        psum = ctx.enter_context(tc.psum_pool(name="psum", bufs=1))
        placed = ctx.enter_context(tc.tile_pool(name="placed", bufs=1))

        def sbuf(name, shape, dtype, tag=None):
            return keep.tile(shape, dtype, name=name, tag=tag or name, align_bytes=DMA_ALIGN)

        def bank(name, shape, number):
            return psum.tile(shape, F32, name=name, tag="bank%d" % number)

        pool_words = sbuf("pool_words", [P, T], U16)
        nc.sync.dma_start(pool_words[:].bitcast(I32), tok_words[0].bitcast(I32))
        offsets = keep.tile([P, I // LIST_GROUP], U16, name="offsets")
        nc.sync.dma_start(offsets[:], offs)
        pool_scales = sbuf("pool_scales", [P, T], U8)
        nc.gpsimd.memset(pool_scales[:].bitcast(I32), 0)
        for f in range(4):
            nc.sync.dma_start(
                pool_scales[f:P:QUADRANT, :].bitcast(I32),
                tok_scales[0, f:SCALE_ROWS:4, :].bitcast(I32),
            )
        mk_rows = mk.rearrange("(p t) m -> p t m", t=PACK)
        mk_raw = []
        for piece, (first, end) in enumerate(MK_PIECES):
            raw = sbuf("mk_raw%d" % piece, [P, PACK, end - first], F32)
            nc.sync.dma_start(raw[:], mk_rows[:, :, first:end])
            mk_raw.append(raw)
        mv_rows = mv.rearrange("(p t) e -> p t e", t=PACK)
        mv_raw = []
        for group in range(GROUPS):
            raw = sbuf("mv_raw%d" % group, [P, PACK, P], F32)
            step = PACK if group == 0 else 2
            for first in range(0, PACK, step):
                nc.sync.dma_start(raw[:, first : first + step], mv_rows[:, first : first + step, group * P : (group + 1) * P])
            mv_raw.append(raw)
        key_scale = sbuf("key_scale", [P, PACK], F32)
        nc.sync.dma_start(key_scale[:], msc.rearrange("(p r) o -> p (r o)", r=PACK))

        identity = sbuf("identity", [P, P], F32)
        make_identity(nc, identity[:])
        table_preload = sbuf("table_preload", [P, 1], F32)
        nc.scalar.activation(table_preload[:], identity[:, 0:1], ACT.Exp)

        token_words = sbuf("token_words", [P, I], U16)
        nc.vector.tensor_copy(token_words[:], pool_words[:].indirect(offsets[:]))
        token_scales = sbuf("token_scales", [P, I], U8)
        nc.vector.tensor_copy(token_scales[:], pool_scales[:].indirect(offsets[:]))

        mk_codes = [sbuf("mk_codes%d" % r, [P, P], U32) for r in range(PACK)]
        mk_scales = [sbuf("mk_scales%d" % r, [P, P], U8) for r in range(PACK)]
        mk_grouped = [sbuf("mk_grouped%d" % pair, [P, 2, P, PACK], BF16) for pair in range(2)]

        def deal_mk(copy, pair, first, end):
            piece = 0 if end <= CUT else 1
            start = piece * CUT
            by_operand = mk_raw[piece][:].rearrange("p t (c r) -> p c t r", r=PACK)
            target = mk_grouped[pair][:, :, first:end, :].rearrange("p r c t -> p c t r")
            copy(target, by_operand[:, first - start : end - start, :, 2 * pair : 2 * pair + 2])

        def quantise_mk(r, first=0, end=P):
            nc.vector.quantize_mx(
                out=mk_codes[r][:, first:end].bitcast(FP8X4),
                scales=mk_scales[r][:, first:end],
                in_=mk_grouped[r // 2][:, r % 2, first:end].rearrange("p c t -> p (c t)"),
            )

        deal_mk(nc.scalar.copy, 0, 0, CUT)
        deal_mk(nc.scalar.copy, 1, 0, WHILE_WAITING)
        deal_mk(nc.vector.tensor_copy, 0, CUT, P - SCALAR_LATE)
        quantise_mk(0, 0, P // 2)
        deal_mk(nc.scalar.copy, 0, P - SCALAR_LATE, P)
        deal_mk(nc.scalar.copy, 1, WHILE_WAITING, CUT)
        quantise_mk(0, P // 2, P)
        deal_mk(nc.vector.tensor_copy, 1, CUT, P)
        quantise_mk(1)
        quantise_mk(2)
        quantise_mk(3)

        mv_grouped = {}

        def interleave_mv(group, copy):
            grouped = sbuf("mv_grouped%d" % group, [P, P, PACK], BF16)
            copy(
                grouped[:].rearrange("p (g n) t -> p g t n", n=RUN),
                mv_raw[group][:].rearrange("p t (g n) -> p g t n", n=RUN),
            )
            mv_grouped[group] = grouped

        for group in range(SCALAR_GROUPS):
            interleave_mv(group, nc.scalar.copy)
        mv_grouped[SCALAR_GROUPS] = sbuf("mv_grouped%d" % SCALAR_GROUPS, [P, P, PACK], BF16, tag="mk_grouped1")
        nc.gpsimd.tensor_scalar(
            mv_grouped[SCALAR_GROUPS][:], mv_raw[SCALAR_GROUPS][:].rearrange("p t e -> p e t"), 1.0, 0.0, ALU.mult, ALU.add
        )

        mv_codes = []
        mv_scales = []

        def quantise_mv(group, on_bytes_of):
            if on_bytes_of is None:
                codes = placed.tile([P, P], U32, name="mv_codes%d" % group, offset=0, align_bytes=DMA_ALIGN)
            else:
                codes = sbuf("mv_codes%d" % group, [P, P], U32, tag=on_bytes_of)
            scales = sbuf("mv_scales%d" % group, [P, P], U8)
            nc.vector.quantize_mx(
                out=codes[:].bitcast(FP8X4), scales=scales[:], in_=mv_grouped[group][:].rearrange("p e t -> p (e t)")
            )
            mv_codes.append(codes[:])
            mv_scales.append(scales[:])

        exps = [sbuf("exps%d" % r, [P, I], F32) for r in range(PACK)]
        row_sum01 = sbuf("row_sum01", [P, 2], F32)
        row_sum2 = sbuf("row_sum2", [P, 1], F32)
        row_sum3 = sbuf("row_sum3", [P, 1], F32)
        row_sum = [row_sum01[:, 0:1], row_sum01[:, 1:2], row_sum2[:], row_sum3[:]]
        for r in range(PACK):
            scores = bank("scores%d" % r, [P, I], r)
            nc.tensor.matmul_mx(
                out=scores[:],
                lhsT=mk_codes[r][:].bitcast(FP8X4),
                lhsT_scale=mk_scales[r][:],
                rhs=token_words[:].bitcast(FP4X4),
                rhs_scale=token_scales[:],
                start=True,
                stop=True,
            )
            neg_max = sbuf("neg_max%d" % r, [P, 1], F32)
            nc.vector.tensor_reduce(neg_max[:], scores[:], AX.X, ALU.max, negate=True)
            nc.scalar.activation(exps[r][:], scores[:], ACT.Exp, bias=neg_max[:], scale=1.0, accum_out=row_sum[r])

        for repeat in range(WARM_UP_PASSES):
            unread = bank("unread%d" % repeat, [P, I], 1)
            nc.tensor.matmul_mx(
                out=unread[:],
                lhsT=mk_codes[repeat][:].bitcast(FP8X4),
                lhsT_scale=mk_scales[repeat][:],
                rhs=token_words[:].bitcast(FP4X4),
                rhs_scale=token_scales[:],
                start=True,
                stop=True,
            )

        row_inv = sbuf("row_inv", [P, PACK], F32)
        shares = [sbuf("shares%d" % r, [P, I], F32) for r in range(PACK)]

        def share_piece(r, first, end):
            if r == 1 and first >= CHUNK:
                return late[:, first - CHUNK : end - CHUNK]
            return shares[r][:, first:end]

        def make_shares(r, first, end):
            nc.vector.tensor_scalar(share_piece(r, first, end), exps[r][:, first:end], row_inv[:, r : r + 1], None, ALU.mult)

        nc.vector.reciprocal(row_inv[:, 0:2], row_sum01[:])
        quantise_mv(0, "neg_max1")
        make_shares(0, 0, I)
        nc.vector.reciprocal(row_inv[:, 2:3], row_sum2[:])
        make_shares(1, 0, CHUNK)
        quantise_mv(1, "row_sum01")
        make_shares(2, 0, CHUNK)
        nc.scalar.activation(shares[2][:, CHUNK:I], exps[2][:, CHUNK:I], ACT.Copy, scale=row_inv[:, 2:3])
        nc.vector.reciprocal(row_inv[:, 3:4], row_sum3[:])
        quantise_mv(2, "neg_max3")
        make_shares(3, 0, CHUNK)
        late = sbuf("late", [P, I - CHUNK], F32, tag="row_sum3")
        make_shares(1, CHUNK, I)
        make_shares(3, CHUNK, I)
        mv_grouped[GROUPS - 1] = sbuf("mv_grouped%d" % (GROUPS - 1), [P, P, PACK], BF16, tag="mk_grouped0")
        nc.gpsimd.tensor_scalar(
            mv_grouped[GROUPS - 1][:], mv_raw[GROUPS - 1][:].rearrange("p t e -> p e t"), 1.0, 0.0, ALU.mult, ALU.add
        )

        scaled = [sbuf("scaled%d" % half, [P, HALF // RUN, PACK, RUN], F32) for half in range(2)]

        def scale_shares(r, first, end):
            half = first // HALF
            target = scaled[half][:, (first - half * HALF) // RUN : (end - half * HALF) // RUN, r, :]
            source = share_piece(r, first, end).rearrange("p (g n) -> p g n", n=RUN)
            nc.scalar.activation(target, source, ACT.Copy, scale=key_scale[:, r : r + 1])

        scale_shares(0, 0, HALF)
        scale_shares(1, 0, CHUNK)
        scale_shares(2, 0, HALF)
        scale_shares(3, 0, CHUNK)
        scale_shares(1, CHUNK, HALF)
        scale_shares(3, CHUNK, HALF)

        turned = []
        for chunk in range(CHUNKS):
            turned_bank = bank("turned%d" % chunk, [P, P], TURNED_BANK + chunk)
            order = (0, 1, 2, 3) if chunk == 0 else (0, 1, 3, 2)
            for step, r in enumerate(order):
                nc.tensor.matmul(
                    turned_bank[:], share_piece(r, chunk * CHUNK, (chunk + 1) * CHUNK), identity[:],
                    start=(step == 0), stop=(step == PACK - 1), is_transpose=True,
                )
            turned.append(turned_bank)
        col_sum0 = sbuf("col_sum0", [P, 1], F32)
        nc.vector.tensor_reduce(col_sum0[:], turned[0][:], AX.X, ALU.add)
        col_inv0 = placed.tile([P, P + 16], F32, name="col_inv0", offset=0, align_bytes=DMA_ALIGN)
        nc.vector.reciprocal(col_inv0[:, 0:1], col_sum0[:])
        col_sum1 = sbuf("col_sum1", [P, 1], F32)
        nc.vector.tensor_reduce(col_sum1[:], turned[1][:], AX.X, ALU.add)
        col_inv1 = sbuf("col_inv1", [P, 1], F32)
        nc.vector.reciprocal(col_inv1[:], col_sum1[:])
        quantise_mv(3, "exps3")
        col_sum23 = sbuf("col_sum23", [P, 2], F32)
        for chunk in range(2, CHUNKS):
            nc.vector.tensor_reduce(col_sum23[:, chunk - 2 : chunk - 1], turned[chunk][:], AX.X, ALU.add)
        for r in range(PACK):
            scale_shares(r, HALF, I)

        spread = []

        def spread_inverse(chunk, inverse):
            spread_bank = bank("spread%d" % chunk, [P, CHUNK], chunk)
            nc.tensor.transpose(spread_bank[:], inverse.to_broadcast([P, P]), identity[:])
            spread.append(spread_bank)

        spread_inverse(0, col_inv0[:, 0:1])
        spread_inverse(1, col_inv1[:])

        out_rows = out.rearrange("(b p) i -> p b i", p=P)
        for chunk in range(CHUNKS):
            slots = slice(chunk * CHUNK, (chunk + 1) * CHUNK)
            weights = sbuf("weights%d" % chunk, [P, CHUNK, PACK], BF16)
            width = CHUNK if chunk == 0 else CHUNK // 2
            for first in range(0, CHUNK, width):
                in_half = (chunk % 2) * CHUNK + first
                inverse_sums = spread[chunk][:, first : first + width].rearrange("p (g n) -> p g n", n=RUN)
                nc.vector.tensor_tensor(
                    weights[:, first : first + width].rearrange("p (g n) r -> p g r n", n=RUN),
                    scaled[chunk // 2][:, in_half // RUN : (in_half + width) // RUN],
                    inverse_sums.unsqueeze(2).to_broadcast([P, width // RUN, PACK, RUN]),
                    ALU.mult,
                )
            if chunk == 0:
                col_inv23 = placed.tile([P, 2], F32, name="col_inv23", offset=4 * P, align_bytes=DMA_ALIGN)
                nc.vector.reciprocal(col_inv23[:], col_sum23[:])
                spread_inverse(2, col_inv23[:, 0:1])
                spread_inverse(3, col_inv23[:, 1:2])
            w_codes = sbuf("w_codes%d" % chunk, [P, CHUNK], U32)
            w_scales = sbuf("w_scales%d" % chunk, [P, CHUNK], U8)
            step = CHUNK // 2 if chunk == CHUNKS - 1 else CHUNK
            for first in range(0, CHUNK, step):
                nc.vector.quantize_mx(
                    out=w_codes[:, first : first + step].bitcast(FP8X4),
                    scales=w_scales[:, first : first + step],
                    in_=weights[:, first : first + step].rearrange("p i r -> p (i r)"),
                )

            def product(target, group):
                nc.tensor.matmul_mx(
                    out=target,
                    lhsT=mv_codes[group].bitcast(FP8X4),
                    lhsT_scale=mv_scales[group],
                    rhs=w_codes[:].bitcast(FP8X4),
                    rhs_scale=w_scales[:],
                    start=True,
                    stop=True,
                )

            for side in range(2):
                result = sbuf("result%d_%d" % (chunk, side), [P, 2, CHUNK], F32)
                if chunk < CHUNKS - 1:
                    sums = bank("sums%d_%d" % (chunk, side), [P, 2, CHUNK], TURNED_BANK + chunk if side == 0 else chunk)
                    for in_bank in range(2):
                        product(sums[:, in_bank, :], 2 * side + in_bank)
                    nc.scalar.copy(result[:], sums[:])
                else:
                    for in_pair, copy in enumerate((nc.vector.tensor_copy, nc.scalar.copy)):
                        number = (TURNED_BANK + chunk, chunk, TURNED_BANK, 0)[2 * side + in_pair]
                        sums = bank("sums%d_%d_%d" % (chunk, side, in_pair), [P, CHUNK], number)
                        product(sums[:], 2 * side + in_pair)
                        copy(result[:, in_pair, :], sums[:])
                nc.sync.dma_start(out_rows[:, 2 * side : 2 * side + 2, slots], result[:])
